import numpy as np, ml_dtypes
CORES = [2,6,10,14,18,22,26,30]
N = 8
BF = ml_dtypes.bfloat16
def gentries(a):
    return np.ascontiguousarray(a.reshape(8, 16, -1).transpose(0, 2, 1)).reshape(8, -1)
def gtable(e):
    e = np.asarray(e); return np.ascontiguousarray(e.reshape(8, -1, 16).transpose(0, 2, 1)).reshape(128, -1).astype(np.int32)
W, LV, B, NB, Q, C = 96, 3, 32, 8, 4, 12096
K = NB * Q
SMIN, SMAX, DM, SH = 4, 88, 12, 9
CUTS = np.array([12, 24]); BASE = np.array([0, 9216, 11520])
def tobf(v):
    return v.astype(np.float32).astype(BF)
def tolists(v):
    return np.stack([gtable(u) for u in v])
def tobox(x, y, s):
    return np.stack([x, y, s], axis=2).reshape(N, 8, 3 * B).astype(np.int32)
def setup_inputs(rng):
    v = rng.integers(0, 256, (N, 128, C), dtype=np.uint8) & rng.integers(0, 256, (N, 128, C), dtype=np.uint8)
    w = rng.integers(-8, 9, (N, 128, 3, NB // 2)); w = np.concatenate([w, -w], axis=3).reshape(N, 128, 3 * NB)
    n = np.arange(K) // Q; hb = 64 // NB
    sx = 4 * (n % 4) + rng.integers(0, 4, (N, 8, K)); sy = hb * (n // 4) + rng.integers(0, hb, (N, 8, K))
    lo = np.append(SMIN, CUTS); hi = np.append(CUTS - 1, SMAX); l = rng.integers(0, LV, (N, 8, B))
    s = rng.integers(lo[l], hi[l] + 1); x = rng.integers(0, W - s + 1); y = rng.integers(0, W - s + 1)
    return {"pyr": tobf(v), "head": tobf(w), "sx": tolists(sx), "sy": tolists(sy), "box": tobox(x, y, s)}
def setup_inputs_ends(rng):
    d = setup_inputs(rng); E = np.concatenate([[SMIN, SMAX], CUTS, CUTS - 1])
    s = E[(np.arange(B) + np.arange(8)[:, None] + np.arange(N)[:, None, None]) % len(E)]
    d["box"] = tobox((W - s) * rng.integers(0, 2, s.shape), (W - s) * rng.integers(0, 2, s.shape), s)
    d["sx"] = tolists(15 * rng.integers(0, 2, (N, 8, K))); d["sy"] = tolists(15 * rng.integers(0, 2, (N, 8, K))); return d
def setup_inputs_slow(rng):
    d = setup_inputs(rng); w = np.zeros((N, 8, 16, 3, NB)); i = np.arange(N)[:, None, None]; g = np.arange(8)[:, None]; c = np.arange(3)
    w[i, g, rng.integers(0, 16, (N, 8, 3)), c, rng.integers(0, NB, (N, 8, 3))] = np.array([-8, -1, 1, 8])[(i + g + c) % 4]
    d["head"] = tobf(w.reshape(N, 128, 3 * NB)); return d
def setup_inputs_twins(rng):
    d = setup_inputs(rng); b = d["box"].reshape(N, 8, 3, B)
    d["box"] = np.ascontiguousarray(np.broadcast_to(b[..., :1], b.shape)).reshape(N, 8, 3 * B); return d
def setup_inputs_push(rng):
    d = setup_inputs(rng); g = 8 * rng.choice(np.array([-1, 1]), (N, 8, 1, 3, 1)); g[:, 0] = 8; g[:, 1] = -8
    d["head"] = tobf(np.broadcast_to(g, (N, 8, 16, 3, NB)).reshape(N, 128, 3 * NB)); return d
def setup_inputs_spread(rng):
    d = setup_inputs(rng); v = np.minimum(rng.integers(0, 256, (N, 8, 16, C), dtype=np.uint8), rng.integers(0, 256, (N, 8, 1, C), dtype=np.uint8))
    d["pyr"] = tobf(v.reshape(N, 128, C)); w = rng.integers(-8, 9, (N, 128, 3 * NB)); d["head"] = tobf(w * (rng.random(w.shape) < 0.25))
    d["sx"] = tolists(rng.integers(0, 16, (N, 8, K))); d["sy"] = tolists(rng.integers(0, 16, (N, 8, K))); return d
def check_inputs(d):
    bad = []
    v = d["pyr"].astype(np.float32)
    if not np.all((v >= 0) & (v <= 255) & (v == np.floor(v))): bad.append("pyr")
    v = d["head"].astype(np.float32)
    if not np.all((v >= -8) & (v <= 8) & (v == np.floor(v))): bad.append("head")
    for a in ("sx", "sy"):
        if not np.all((d[a] >= 0) & (d[a] <= 15)): bad.append(a)
    b = d["box"].astype(np.int64).reshape(N, 8, 3, B); x, y, s = b[:, :, 0], b[:, :, 1], b[:, :, 2]
    if not np.all((s >= SMIN) & (s <= SMAX)): bad.append("size")
    if not np.all((x >= 0) & (y >= 0) & (x + s <= W) & (y + s <= W)): bad.append("box")
    return bad
def reference(pyr, head, sx, sy, box):
    P = [pyr[q].astype(np.float32).reshape(8, 16, C) for q in range(N)]
    H = [head[q].astype(np.float32).astype(np.int64).reshape(8, 16, 3, NB) for q in range(N)]
    ax = [gentries(sx[q]).astype(np.int64)[:, None, :] for q in range(N)]; ay = [gentries(sy[q]).astype(np.int64)[:, None, :] for q in range(N)]
    feat = np.zeros((N, 128, NB * B), BF); trail = np.zeros((N, 8, N, 3, B), np.float32)
    g = np.arange(8)[:, None, None]; ch = np.arange(16)[None, :, None]
    for r in range(N):
        b = box[r].astype(np.int64).reshape(8, 3, B); x, y, s = b[:, 0], b[:, 1], b[:, 2]
        for h in range(N):
            q = (r + h) % N
            l = np.zeros((8, B), np.int64)
            for t in CUTS: l = l + (s >= t)
            u = (16 * x[:, :, None] + ax[q] * s[:, :, None]) >> (4 + l[:, :, None])
            v = (16 * y[:, :, None] + ay[q] * s[:, :, None]) >> (4 + l[:, :, None])
            at = BASE[l][:, :, None] + v * (W >> l)[:, :, None] + u
            e = P[q][g, ch, at.reshape(8, 1, B * K)]
            m = np.max(e.reshape(8, 16, B, NB, Q), axis=4)
            d = np.einsum("gcbn,gcdn->gdb", m.astype(np.int64), H[q]) >> SH
            d = np.minimum(np.maximum(d, -DM), DM)
            s = np.minimum(np.maximum(s + d[:, 2], SMIN), SMAX)
            x = np.minimum(np.maximum(x + d[:, 0], 0), W - s)
            y = np.minimum(np.maximum(y + d[:, 1], 0), W - s)
            trail[r, :, h] = np.stack([x, y, s], axis=1)
        feat[r] = m.transpose(0, 1, 3, 2).reshape(128, NB * B).astype(BF)
    return {"feat": feat, "trail": trail.reshape(N, 8, 3 * N * B)}

@@ -1,0 +1,310 @@
+from concourse.mybir import AluOpType as Op, ActivationFunctionType as Act
+
+NH = 2
+NV = 8
+WS, WL = 48, 176
+DT, FT = 16, 48
+KR = 65
+
+
+def slot(h, j):
+    per = 7 * WS + 2 * WL
+    return h * per + ((j + 1) * WS if j <= 6 else 7 * WS + WL)
+
+
+SCRATCH = {
+    "win": ("sbuf", [128, 18432], "bfloat16"),
+    "s1": ("sbuf", [128, 48, 2, 48], "bfloat16"),
+    "s2": ("sbuf", [128, 24, 4, 24], "bfloat16"),
+    "hd": ("sbuf", [128, 24], "bfloat16"),
+    "h4": ("sbuf", [128, 32], "bfloat16"),
+    "wt": ("sbuf", [128, 256], "bfloat16"),
+    "ints": ("sbuf", [128, 160], "int32"),
+    "smb": ("sbuf", [128, 160], "bfloat16"),
+    "dio": ("sbuf", [128, 128], "float32"),
+    "dio2": ("sbuf", [128, 128], "float32"),
+    "ident": ("sbuf", [128, 128], "bfloat16"),
+    "iy": ("sbuf", [128, 128], "bfloat16"),
+    "ix": ("sbuf", [128, 128], "bfloat16"),
+    "ig": ("sbuf", [128, 128], "bfloat16"),
+    "i8": ("sbuf", [128, 128], "bfloat16"),
+    "ones": ("sbuf", [128, 128], "bfloat16"),
+    "nid": ("sbuf", [128, 8], "bfloat16"),
+    "mkt": ("sbuf", [128, 128], "bfloat16"),
+    "mkc": ("sbuf", [128, 8], "float32"),
+    "mk": ("sbuf", [128, 8], "float32"),
+    "rep": ("sbuf", [128, 32], "bfloat16"),
+    "sxy": ("sbuf", [128, 64], "bfloat16"),
+    "cb1": ("sbuf", [128, 16], "bfloat16"),
+    "cb3": ("sbuf", [128, 32], "bfloat16"),
+    "cin": ("sbuf", [128, 4], "bfloat16"),
+    "c48": ("sbuf", [128, 48], "float32"),
+    "sgc": ("sbuf", [128, 40], "float32"),
+    "sgo": ("sbuf", [128, 16], "float32"),
+    "dt0": ("sbuf", [128, 32], "bfloat16"),
+    "est": ("sbuf", [128, 8], "bfloat16"),
+    "eland": ("sbuf", [128, 8], "bfloat16"),
+    "msg": ("sbuf", [128, 2 * (7 * WS + 2 * WL)], "bfloat16"),
+    "fo": ("sbuf", [128, 8, 32], "bfloat16"),
+    "tr": ("sbuf", [128, 24, 32], "float32"),
+}
+for _h in range(NH):
+    SCRATCH["q%d" % _h] = ("sbuf", [128, 64], "bfloat16")
+    SCRATCH["tau%d" % _h] = ("sbuf", [128, 32], "bfloat16")
+    SCRATCH["sum%d" % _h] = ("sbuf", [128, 1], "float32")
+    SCRATCH["base%d" % _h] = ("sbuf", [128, 1], "float32")
+    SCRATCH["off%d" % _h] = ("sbuf", [128, 32], "uint16")
+    SCRATCH["ga%d" % _h] = ("sbuf", [128, 128], "bfloat16")
+    SCRATCH["gb%d" % _h] = ("sbuf", [128, 128], "bfloat16")
+    for _n in "ABC":
+        SCRATCH["ps%s%d" % (_n, _h)] = ("psum", [128, 512], "float32")
+
+SEMAPHORES = ["v", "a", "pe", "gp", "lds", "ld1", "ld0", "early", "loc", "st1", "st2"] + \
+             ["arr%d_%d" % (h, j) for h in range(NH) for j in range(NV)]
+
+
+def rank_program(g, core, T, topo):
+    rank = T.rank_of(core)
+    if rank is None:
+        return
+    n = len(T.cores)
+    nxt, prv = T.cores[(rank + 1) % n], T.cores[(rank - 1) % n]
+    rid, pid, _ = topo.addr(nxt)
+    mask = topo.mask(core, nxt)
+    n_out, n_in = len(topo.engines(core, nxt)), len(topo.engines(prv, core))
+
+    Q = {"v": g.vector, "a": g.scalar, "pe": g.tensor, "gp": g, "sy": g.sync}
+    cnt = {"v": 0, "a": 0, "pe": 0, "gp": 0, "loc": 0}
+    seen = {}
+
+    def wait(q, *tickets):
+        for t in tickets:
+            if t is not None and seen.get((q, t[0]), 0) < t[1]:
+                Q[q].wait_ge(T.sem[t[0]], t[1])
+                seen[(q, t[0])] = t[1]
+
+    def done(q, inst):
+        inst.then_inc(T.sem[q], 1)
+        cnt[q] += 1
+        return (q, cnt[q])
+
+    def ts(out, in0, s1, s2, op0, op1=None, deps=()):
+        wait("v", *deps)
+        if op1 is None:
+            return done("v", g.vector.tensor_scalar(out, in0, s1, None, op0))
+        return done("v", g.vector.tensor_scalar(out, in0, s1, s2, op0, op1))
+
+    def tt(out, a, b, op, deps=()):
+        wait("v", *deps)
+        return done("v", g.vector.tensor_tensor(out, a, b, op))
+
+    def cp(out, a, deps=()):
+        wait("v", *deps)
+        return done("v", g.vector.tensor_copy(out, a))
+
+    def fill(ap, c, deps=()):
+        wait("v", *deps)
+        return done("v", g.vector.memset(ap, c))
+
+    def mm(out, lhsT, rhs, start, stop, deps=()):
+        wait("pe", *deps)
+        return done("pe", g.tensor.matmul(out, lhsT, rhs, start, stop))
+
+    def act(out, in_, func, deps=(), **kw):
+        wait("a", *deps)
+        return done("a", g.scalar.activation(out, in_, func, **kw))
+
+    def send(dst, src, sem, deps):
+        wait("gp", *deps)
+        g.remote_dma(dst, src, T.sem[sem], T.sem.loc, pid, rid, mask)
+        cnt["loc"] += n_out
+
+    M = T.msg
+    pA = [T["psA%d" % h] for h in range(NH)]
+    pB = [T["psB%d" % h] for h in range(NH)]
+    pC = [T["psC%d" % h] for h in range(NH)]
+
+    g.scalar.dma_start(T.ints[0:8, 64:160], T.box[:]).then_inc(T.sem.lds, 16)
+    g.scalar.dma_start(T.ints[0:8, 0:32], T.sy[:]).then_inc(T.sem.lds, 16)
+    g.sync.dma_start(T.hd[:], T.head[:]).then_inc(T.sem.lds, 16)
+    g.sync.dma_start(T.ints[0:8, 32:64], T.sx[:]).then_inc(T.sem.lds, 16)
+    g.sync.dma_start(T.win[:, 0:2880], T.pyr[:, 9216:12096]).then_inc(T.sem.ld1, 16)
+    g.sync.dma_start(T.win[:, 9216:18432], T.pyr[:, 0:9216]).then_inc(T.sem.ld0, 16)
+    lds, ld1, ld0 = ("lds", 64), ("ld1", 16), ("ld0", 16)
+
+    io1 = done("gp", g.iota(T.dio[:], [[-1, 128]], 0, 1, allow_small_or_imprecise_dtypes=True))
+    io2 = done("gp", g.iota(T.dio2[0:8, :], [[1, 8], [0, 16]], 0, -1, allow_small_or_imprecise_dtypes=True))
+    fill(T.ones[:], 1.0)
+    fill(T.rep[0:64, :], 0.0)
+    fill(T.rep[64:KR, :], -1.0)
+    fill(T.dt0[0:KR, :], 0.0)
+    fill(T.cb1[0:32, :], 0.75)
+    fill(T.cb1[32:64, :], -2.0 ** -9)
+    fill(T.cb1[64:96, :], 2.0 ** -18)
+    tid = ts(T.ident[:], T.dio[:], 0.0, None, Op.is_equal, deps=[io1])
+    t = ts(T.mkc[:], T.dio[:, 0:128:16], 0.0, 15.0, Op.max, Op.min)
+    ts(T.nid[0:8, :], T.dio[0:8, 0:8], 0.0, -1.0, Op.is_equal, Op.mult)
+    ts(T.mkt[0:8, :], T.dio2[0:8, :], 0.0, None, Op.is_equal, deps=[io2])
+    tmk = tt(T.mk[:], T.mkc[:], T.dio[:, 0:128:16], Op.is_equal, [t])
+    cp(T.rep[0:16, 0:16], T.ident[0:16, 0:16])
+    cp(T.rep[32:48, 16:32], T.ident[32:48, 32:48])
+    fill(T.cb1[32:64, 3:16:4], 2.0 ** -9)
+    fill(T.cb1[64:96, 3:16:4], -2.0 ** -18)
+    fill(T.cb3[0:32, :], 12.5)
+    fill(T.cb3[32:64, :], 7.0 / 2048)
+    fill(T.cin[0:1, 0:2], -0.5)
+    fill(T.cin[0:1, 2:3], 0.0)
+    fill(T.cin[0:1, 3:4], 11.5)
+    fill(T.sgc[:, 0:33], -23.5 / 8)
+    fill(T.sgc[:, 33:35], -11.5 / 8)
+    fill(T.sgc[:, 35:40], -1000.0)
+    for h in range(NH):
+        fill(M[:, slot(h, -1):slot(h, -1) + DT], 24.0)
+    for buf, c in ((T.iy, -12.0), (T.ix, -0.125), (T.ig, 5.0 / 64), (T.i8, 8.0)):
+        tis = act(buf[:], T.ident[:], Act.Copy, [tid], scale=c)
+
+    tb = ts(T.smb[0:8, 64:160], T.ints[0:8, 64:160], 0.125, None, Op.mult, deps=[lds])
+    tsx = ts(T.smb[0:8, 0:64], T.ints[0:8, 0:64], 0.5, None, Op.mult)
+    for h in range(NH):
+        for e in range(4):
+            for blk in range(2):
+                c0 = 64 + 32 * min(e, 2) + 16 * h
+                src = T.nid if e == 3 else T.ident
+                tm0 = mm(pA[0][32 * blk:32 * blk + 16, 16 * h + e:16 * h + 16:4], T.smb[0:8, c0:c0 + 16],
+                         src[0:8, blk:8:2], True, True, [tb])
+    for tbl in range(2):
+        for s in range(4):
+            for kk in range(2):
+                c0 = 32 * tbl + 8 * s + 4 * kk
+                tm1 = mm(pC[1][:, c0:c0 + 4], T.mkt[0:8, :], T.smb[0:8, 32 * tbl + 2 * s + kk:32 * tbl + 32:8],
+                         True, True, [tsx])
+    act(T.h4[:, 0:24], T.hd[:], Act.Copy, [lds], scale=1.0 / 4096)
+    t = act(T.h4[:, 24:32], T.hd[:, 16:24], Act.Copy, scale=-1.0 / 4096)
+    for gi in range(8):
+        c0 = 128 * (gi % 2) + 32 * (gi // 2)
+        act(T.wt[:, c0:c0 + 32], T.h4[:], Act.Identity, [t, tmk], scale=T.mk[:, gi:gi + 1])
+    cp(T.dt0[0:16, :], pA[0][0:16, 0:32], [tm0])
+    td0 = cp(T.dt0[32:48, :], pA[0][32:48, 0:32])
+    tsxy = cp(T.sxy[:], pC[1][:, 0:64], [tm1])
+
+    last = [{"v1": td0, "v5": tsxy, "xy": None} for _ in range(NH)]
+
+    def open_groups(h):
+        mm(pC[h][:, 0:32], T.ones[0:64, :], T.cb3[0:64, :], True, False, [last[h]["v5"], last[h]["v1"]])
+        mm(pA[h][0:48, 0:16], T.ones[0:96, 0:48], T.cb1[0:96, :], True, False)
+
+    def update(h, first, dts, st, deps):
+        mm(pB[h][:, 0:4], first[0], first[1], True, False, list(deps) + [last[h]["xy"]])
+        for qd in range(4):
+            t = mm(pB[h][32 * qd:32 * qd + 32, 0:4], T.rep[0:KR, :], dts(qd), False, True)
+        return ts(st(2, 4), pB[h][:, 2:4], 0.5, 11.0, Op.max, Op.min, deps=[t])
+
+    def clamp_xy(h, st, v2):
+        last[h]["xy"] = ts(st(0, 2), pB[h][:, 0:2], -0.5, st(3, 4), Op.max, Op.min, deps=[v2])
+        return last[h]["xy"]
+
+    def level(h, st, v2):
+        tg = act(T["tau%d" % h][:], T.sgc[:, 0:32], Act.Sign, [v2], bias=st(2, 3))
+        return tg, act(T.sgo[:, 8 * h:8 * h + 8], T.sgc[:, 32:40], Act.Sign, bias=st(2, 3),
+                       accum_out=T["sum%d" % h][:])
+
+    def steps(h, st, v2, tg):
+        qb = T["q%d" % h]
+        tq = ts(qb[:], T.sxy[:], st(2, 3), 131.53125, Op.mult, Op.add, deps=[v2])
+        txy = clamp_xy(h, st, v2)
+        mm(pC[h][:, 0:32], T.iy[:], qb[:, 0:32], False, False, [tq, tis])
+        mm(pC[h][:, 0:32], T.ix[:], qb[:, 32:64], False, False)
+        m3 = mm(pC[h][:, 0:32], T.ig[:], T["tau%d" % h][:], False, True, [tg])
+        return txy, m3
+
+    def offsets(h, st, txy, m3, sg):
+        bs = T["base%d" % h]
+        v4 = ts(bs[:], st(1, 2), -96.0, st(0, 1), Op.mult, Op.subtract, deps=[txy])
+        last[h]["v5"] = ts(T["off%d" % h][:], pC[h][:, 0:32], bs[:], T["sum%d" % h][:], Op.add, Op.mult,
+                           deps=[v4, m3, sg])
+
+    def visit(h, j, ready):
+        off, ga, gb = T["off%d" % h], T["ga%d" % h], T["gb%d" % h]
+        s0 = slot(h, j - 1)
+        deps = [last[h]["v5"]] + ready
+        ta = act(ga[:, 64:128], T.win[:].indirect(off[:, 4:8]), Act.Copy, deps)
+        t = cp(ga[:, 0:64], T.win[:].indirect(off[:, 0:4]), deps)
+        t = tt(gb[:], T.win[:].indirect(off[:, 8:16]), ga[:], Op.max, [t, ta])
+        t = tt(ga[:], T.win[:].indirect(off[:, 16:24]), gb[:], Op.max, [t])
+        fb, f0 = (M, s0 + FT) if j == NV - 1 else (gb, 0)
+        t = tt(fb[:, f0:f0 + 128], T.win[:].indirect(off[:, 24:32]), ga[:], Op.max, [t])
+        for b in range(7, -1, -1):
+            for blk in range(2):
+                wd = 32 if b == 0 and blk == 0 else 16
+                m1 = mm(pA[h][32 * blk:32 * blk + wd, 0:16], fb[:, f0 + 16 * b:f0 + 16 * b + wd],
+                        T.wt[:, 128 * blk + b:128 * blk + 128:8], False, b == 0, [t])
+        last[h]["v1"] = ts(M[0:48, s0:s0 + DT], pA[h][0:48, 0:16], 22.5, 25.5, Op.max, Op.min, deps=[m1])
+        w = WL if j == NV - 1 else DT + 4 * j
+        send(M[:, slot(h, j):slot(h, j) + w], M[:, s0:s0 + w], "arr%d_%d" % (h, j), [last[h]["v1"]])
+
+    sts = [lambda a, b, h=h: T.est[:, 4 * h + a:4 * h + b] for h in range(NH)]
+    v2s, mids, sgs = [], [], []
+    for h in range(NH):
+        v2s.append(update(h, (T.ones[0:1, :], T.cin[0:1, :]), lambda qd: T.dt0[0:KR, 16 * h + 4 * qd:16 * h + 4 * qd + 4],
+                          sts[h], [td0]))
+    for h in range(NH):
+        open_groups(h)
+    for h in range(NH):
+        sgs.append(level(h, sts[h], v2s[h]))
+        mids.append(steps(h, sts[h], v2s[h], sgs[h][0]))
+    send(T.eland[:], T.est[:], "early", [mids[1][0]])
+    for h in range(NH):
+        offsets(h, sts[h], mids[h][0], mids[h][1], sgs[h][1])
+    for k in range(4):
+        t = act(T.s2[:, :, k, :], T.win[:, 2304:2880], Act.Copy, [ld1])
+    ea = act(T.win[:, 2304:4608], T.s2[:], Act.Copy, [t])
+    for k in range(2):
+        t = cp(T.s1[:, :, k, :], T.win[:, 0:2304], [ld1])
+    ev = cp(T.win[:, 4608:9216], T.s1[:], [t])
+    for h in range(NH):
+        visit(h, 0, [ld0, ld1, ea, ev])
+    for h in range(NH):
+        fill(M[:, slot(h, 6) + 40:slot(h, 6) + FT], 0.0)
+    fill(T.c48[0:8, 0:32], 4.0)
+    fill(T.c48[0:8, 32:48], 0.0)
+
+    def arrival(h, j):
+        s = slot(h, j)
+        prev = T.eland[:, 4 * h:4 * h + 4] if j == 0 else M[:, s + DT + 4 * j - 4:s + DT + 4 * j]
+        st = lambda a, b: M[:, s + DT + 4 * j + a:s + DT + 4 * j + b]
+        deps = [("arr%d_%d" % (h, j), n_in)] + ([("early", n_in)] if j == 0 else [])
+        return st, update(h, (T.ident[:], prev), lambda qd: M[0:KR, s + 4 * qd:s + 4 * qd + 4], st, deps)
+
+    for j in range(NV - 1):
+        for h in range(NH):
+            open_groups(h)
+            st, v2 = arrival(h, j)
+            tg, sg = level(h, st, v2)
+            txy, m3 = steps(h, st, v2, tg)
+            offsets(h, st, txy, m3, sg)
+            visit(h, j + 1, [])
+
+    for h in range(NH):
+        s = slot(h, NV - 1)
+        tf = act(T.fo[:, :, 16 * h:16 * h + 16], M[:, s + FT:s + WL], Act.Copy, [("arr%d_%d" % (h, NV - 1), n_in)])
+        if h == NH - 1:
+            wait("sy", tf)
+            g.sync.dma_start(T.feat[:], T.fo[:]).then_inc(T.sem.st1, 16)
+        st, v2 = arrival(h, NV - 1)
+        txy = clamp_xy(h, st, v2)
+        for e in range(3):
+            for b in range(16):
+                th = mm(pA[h][0:8, 128 * e + b:128 * e + 112:16], T.i8[:, b:128:16], M[:, s + DT + e:s + DT + 28:4],
+                        True, True, [last[h]["v1"]])
+        for b in range(16):
+            tl = mm(pC[h][0:8, b:48:16], T.i8[:, b:128:16], st(0, 3), True, True, [txy])
+        for e in range(3):
+            te = act(T.tr[0:8, e:21:3, 16 * h:16 * h + 16], pA[h][0:8, 128 * e:128 * e + 112], Act.Identity, [th],
+                     bias=4.0 if e < 2 else 0.0)
+        tz = tt(T.tr[0:8, 21:24, 16 * h:16 * h + 16], pC[h][0:8, 0:48], T.c48[0:8, :], Op.add, [tl])
+    wait("sy", te)
+    g.sync.dma_start(T.trail[:, 0:672], T.tr[0:8, 0:21, :]).then_inc(T.sem.st1, 16)
+    wait("a", tz)
+    g.scalar.dma_start(T.trail[:, 672:768], T.tr[0:8, 21:24, :]).then_inc(T.sem.st2, 16)
+    wait("gp", ("loc", cnt["loc"]), ("v", cnt["v"]), ("a", cnt["a"]), ("pe", cnt["pe"]), ("gp", cnt["gp"]),
+         ("st1", 32), ("st2", 16))

@@ -12,50 +12,17 @@ def slot(h, j):
     return h * per + ((j + 1) * WS if j <= 6 else 7 * WS + WL)
 
 
-SCRATCH = {
-    "win": ("sbuf", [128, 18432], "bfloat16"),
-    "s1": ("sbuf", [128, 48, 2, 48], "bfloat16"),
-    "s2": ("sbuf", [128, 24, 4, 24], "bfloat16"),
-    "hd": ("sbuf", [128, 24], "bfloat16"),
-    "h4": ("sbuf", [128, 32], "bfloat16"),
-    "wt": ("sbuf", [128, 256], "bfloat16"),
-    "ints": ("sbuf", [128, 160], "int32"),
-    "smb": ("sbuf", [128, 160], "bfloat16"),
-    "dio": ("sbuf", [128, 128], "float32"),
-    "dio2": ("sbuf", [128, 128], "float32"),
-    "ident": ("sbuf", [128, 128], "bfloat16"),
-    "iy": ("sbuf", [128, 128], "bfloat16"),
-    "ix": ("sbuf", [128, 128], "bfloat16"),
-    "ig": ("sbuf", [128, 128], "bfloat16"),
-    "i8": ("sbuf", [128, 128], "bfloat16"),
-    "ones": ("sbuf", [128, 128], "bfloat16"),
-    "nid": ("sbuf", [128, 8], "bfloat16"),
-    "mkt": ("sbuf", [128, 128], "bfloat16"),
-    "mkc": ("sbuf", [128, 8], "float32"),
-    "mk": ("sbuf", [128, 8], "float32"),
-    "rep": ("sbuf", [128, 32], "bfloat16"),
-    "sxy": ("sbuf", [128, 64], "bfloat16"),
-    "cb1": ("sbuf", [128, 16], "bfloat16"),
-    "cb3": ("sbuf", [128, 32], "bfloat16"),
-    "cin": ("sbuf", [128, 4], "bfloat16"),
-    "c48": ("sbuf", [128, 48], "float32"),
-    "sgc": ("sbuf", [128, 40], "float32"),
-    "sgo": ("sbuf", [128, 16], "float32"),
-    "dt0": ("sbuf", [128, 32], "bfloat16"),
-    "est": ("sbuf", [128, 8], "bfloat16"),
-    "eland": ("sbuf", [128, 8], "bfloat16"),
-    "msg": ("sbuf", [128, 2 * (7 * WS + 2 * WL)], "bfloat16"),
-    "fo": ("sbuf", [128, 8, 32], "bfloat16"),
-    "tr": ("sbuf", [128, 24, 32], "float32"),
-}
+SCRATCH = {"s1": ("sbuf", [128, 48, 2, 48], "bfloat16"), "s2": ("sbuf", [128, 24, 4, 24], "bfloat16"),
+           "fo": ("sbuf", [128, 8, 32], "bfloat16"), "tr": ("sbuf", [128, 24, 32], "float32"),
+           "ints": ("sbuf", [128, 160], "int32")}
+for _n, _c in dict(win=18432, hd=24, h4=32, wt=256, smb=160, ident=128, iy=128, ix=128, ig=128, i8=128, ones=128, nid=8,
+                   mkt=128, rep=32, sxy=64, cb1=16, cb3=32, cin=4, dt0=32, est=8, eland=8, msg=2 * (7 * WS + 2 * WL),
+                   q0=64, q1=64, tau0=32, tau1=32, ga0=128, ga1=128, gb0=128, gb1=128).items():
+    SCRATCH[_n] = ("sbuf", [128, _c], "bfloat16")
+for _n, _c in dict(dio=128, dio2=128, mkc=8, mk=8, c48=48, sgc=40, sgo=16, sum0=1, sum1=1, base0=1, base1=1).items():
+    SCRATCH[_n] = ("sbuf", [128, _c], "float32")
 for _h in range(NH):
-    SCRATCH["q%d" % _h] = ("sbuf", [128, 64], "bfloat16")
-    SCRATCH["tau%d" % _h] = ("sbuf", [128, 32], "bfloat16")
-    SCRATCH["sum%d" % _h] = ("sbuf", [128, 1], "float32")
-    SCRATCH["base%d" % _h] = ("sbuf", [128, 1], "float32")
     SCRATCH["off%d" % _h] = ("sbuf", [128, 32], "uint16")
-    SCRATCH["ga%d" % _h] = ("sbuf", [128, 128], "bfloat16")
-    SCRATCH["gb%d" % _h] = ("sbuf", [128, 128], "bfloat16")
     for _n in "ABC":
         SCRATCH["ps%s%d" % (_n, _h)] = ("psum", [128, 512], "float32")
 
@@ -189,9 +156,11 @@ def rank_program(g, core, T, topo):
 
     last = [{"v1": td0, "v5": tsxy, "xy": None} for _ in range(NH)]
 
-    def open_groups(h):
-        mm(pC[h][:, 0:32], T.ones[0:64, :], T.cb3[0:64, :], True, False, [last[h]["v5"], last[h]["v1"]])
-        mm(pA[h][0:48, 0:16], T.ones[0:96, 0:48], T.cb1[0:96, :], True, False)
+    def open_c(h):
+        mm(pC[h][:, 0:32], T.ones[0:64, :], T.cb3[0:64, :], True, False, [last[h]["v5"]])
+
+    def open_a(h):
+        mm(pA[h][0:48, 0:16], T.ones[0:96, 0:48], T.cb1[0:96, :], True, False, [last[h]["v1"]])
 
     def update(h, first, dts, st, deps):
         mm(pB[h][:, 0:4], first[0], first[1], True, False, list(deps) + [last[h]["xy"]])
@@ -227,17 +196,22 @@ def rank_program(g, core, T, topo):
         off, ga, gb = T["off%d" % h], T["ga%d" % h], T["gb%d" % h]
         s0 = slot(h, j - 1)
         deps = [last[h]["v5"]] + ready
-        ta = act(ga[:, 64:128], T.win[:].indirect(off[:, 4:8]), Act.Copy, deps)
-        t = cp(ga[:, 0:64], T.win[:].indirect(off[:, 0:4]), deps)
-        t = tt(gb[:], T.win[:].indirect(off[:, 8:16]), ga[:], Op.max, [t, ta])
-        t = tt(ga[:], T.win[:].indirect(off[:, 16:24]), gb[:], Op.max, [t])
+        open_a(h)
+        if j < NV - 1:
+            open_c(h)
         fb, f0 = (M, s0 + FT) if j == NV - 1 else (gb, 0)
-        t = tt(fb[:, f0:f0 + 128], T.win[:].indirect(off[:, 24:32]), ga[:], Op.max, [t])
+        ta = act(ga[:, 0:64], T.win[:].indirect(off[:, 0:4]), Act.Copy, deps)
+        tk = [ta, cp(ga[:, 64:128], T.win[:].indirect(off[:, 4:8]), deps)]
+        for s, (src, dst, d0) in enumerate(((ga, gb, 0), (gb, ga, 0), (ga, fb, f0))):
+            for k in (1, 0):
+                c = 8 * s + 8 + 4 * k
+                tk[k] = tt(dst[:, d0 + 64 * k:d0 + 64 * k + 64], T.win[:].indirect(off[:, c:c + 4]),
+                           src[:, 64 * k:64 * k + 64], Op.max, [tk[k]])
         for b in range(7, -1, -1):
             for blk in range(2):
                 wd = 32 if b == 0 and blk == 0 else 16
                 m1 = mm(pA[h][32 * blk:32 * blk + wd, 0:16], fb[:, f0 + 16 * b:f0 + 16 * b + wd],
-                        T.wt[:, 128 * blk + b:128 * blk + 128:8], False, b == 0, [t])
+                        T.wt[:, 128 * blk + b:128 * blk + 128:8], False, b == 0, [tk[b // 4]])
         last[h]["v1"] = ts(M[0:48, s0:s0 + DT], pA[h][0:48, 0:16], 22.5, 25.5, Op.max, Op.min, deps=[m1])
         w = WL if j == NV - 1 else DT + 4 * j
         send(M[:, slot(h, j):slot(h, j) + w], M[:, s0:s0 + w], "arr%d_%d" % (h, j), [last[h]["v1"]])
@@ -248,7 +222,7 @@ def rank_program(g, core, T, topo):
         v2s.append(update(h, (T.ones[0:1, :], T.cin[0:1, :]), lambda qd: T.dt0[0:KR, 16 * h + 4 * qd:16 * h + 4 * qd + 4],
                           sts[h], [td0]))
     for h in range(NH):
-        open_groups(h)
+        open_c(h)
     for h in range(NH):
         sgs.append(level(h, sts[h], v2s[h]))
         mids.append(steps(h, sts[h], v2s[h], sgs[h][0]))
@@ -277,7 +251,6 @@ def rank_program(g, core, T, topo):
 
     for j in range(NV - 1):
         for h in range(NH):
-            open_groups(h)
             st, v2 = arrival(h, j)
             tg, sg = level(h, st, v2)
             txy, m3 = steps(h, st, v2, tg)

@@ -162,11 +162,14 @@ def rank_program(g, core, T, topo):
     def open_a(h):
         mm(pA[h][0:48, 0:16], T.ones[0:96, 0:48], T.cb1[0:96, :], True, False, [last[h]["v1"]])
 
-    def update(h, first, dts, st, deps):
+    def add_moves(h, first, dts, deps):
         mm(pB[h][:, 0:4], first[0], first[1], True, False, list(deps) + [last[h]["xy"]])
         for qd in range(4):
             t = mm(pB[h][32 * qd:32 * qd + 32, 0:4], T.rep[0:KR, :], dts(qd), False, True)
-        return ts(st(2, 4), pB[h][:, 2:4], 0.5, 11.0, Op.max, Op.min, deps=[t])
+        return t
+
+    def clamp_s(h, st, m2):
+        return ts(st(2, 4), pB[h][:, 2:4], 0.5, 11.0, Op.max, Op.min, deps=[m2])
 
     def clamp_xy(h, st, v2):
         last[h]["xy"] = ts(st(0, 2), pB[h][:, 0:2], -0.5, st(3, 4), Op.max, Op.min, deps=[v2])
@@ -177,14 +180,14 @@ def rank_program(g, core, T, topo):
         return tg, act(T.sgo[:, 8 * h:8 * h + 8], T.sgc[:, 32:40], Act.Sign, bias=st(2, 3),
                        accum_out=T["sum%d" % h][:])
 
-    def steps(h, st, v2, tg):
+    def sample_steps(h, st, v2):
+        return ts(T["q%d" % h][:], T.sxy[:], st(2, 3), 131.53125, Op.mult, Op.add, deps=[v2])
+
+    def mix(h, tq, tg):
         qb = T["q%d" % h]
-        tq = ts(qb[:], T.sxy[:], st(2, 3), 131.53125, Op.mult, Op.add, deps=[v2])
-        txy = clamp_xy(h, st, v2)
         mm(pC[h][:, 0:32], T.iy[:], qb[:, 0:32], False, False, [tq, tis])
         mm(pC[h][:, 0:32], T.ix[:], qb[:, 32:64], False, False)
-        m3 = mm(pC[h][:, 0:32], T.ig[:], T["tau%d" % h][:], False, True, [tg])
-        return txy, m3
+        return mm(pC[h][:, 0:32], T.ig[:], T["tau%d" % h][:], False, True, [tg])
 
     def offsets(h, st, txy, m3, sg):
         bs = T["base%d" % h]
@@ -192,14 +195,16 @@ def rank_program(g, core, T, topo):
         last[h]["v5"] = ts(T["off%d" % h][:], pC[h][:, 0:32], bs[:], T["sum%d" % h][:], Op.add, Op.mult,
                            deps=[v4, m3, sg])
 
-    def visit(h, j, ready):
+    def feats(h, j):
+        return (M, slot(h, j - 1) + FT) if j == NV - 1 else (T["gb%d" % h], 0)
+
+    def gathers(h, j, ready):
         off, ga, gb = T["off%d" % h], T["ga%d" % h], T["gb%d" % h]
-        s0 = slot(h, j - 1)
         deps = [last[h]["v5"]] + ready
         open_a(h)
         if j < NV - 1:
             open_c(h)
-        fb, f0 = (M, s0 + FT) if j == NV - 1 else (gb, 0)
+        fb, f0 = feats(h, j)
         ta = act(ga[:, 0:64], T.win[:].indirect(off[:, 0:4]), Act.Copy, deps)
         tk = [ta, cp(ga[:, 64:128], T.win[:].indirect(off[:, 4:8]), deps)]
         for s, (src, dst, d0) in enumerate(((ga, gb, 0), (gb, ga, 0), (ga, fb, f0))):
@@ -207,11 +212,19 @@ def rank_program(g, core, T, topo):
                 c = 8 * s + 8 + 4 * k
                 tk[k] = tt(dst[:, d0 + 64 * k:d0 + 64 * k + 64], T.win[:].indirect(off[:, c:c + 4]),
                            src[:, 64 * k:64 * k + 64], Op.max, [tk[k]])
+        return tk
+
+    def head(h, j, tk):
+        fb, f0 = feats(h, j)
         for b in range(7, -1, -1):
             for blk in range(2):
                 wd = 32 if b == 0 and blk == 0 else 16
                 m1 = mm(pA[h][32 * blk:32 * blk + wd, 0:16], fb[:, f0 + 16 * b:f0 + 16 * b + wd],
                         T.wt[:, 128 * blk + b:128 * blk + 128:8], False, b == 0, [tk[b // 4]])
+        return m1
+
+    def moves_out(h, j, m1):
+        s0 = slot(h, j - 1)
         last[h]["v1"] = ts(M[0:48, s0:s0 + DT], pA[h][0:48, 0:16], 22.5, 25.5, Op.max, Op.min, deps=[m1])
         w = WL if j == NV - 1 else DT + 4 * j
         send(M[:, slot(h, j):slot(h, j) + w], M[:, s0:s0 + w], "arr%d_%d" % (h, j), [last[h]["v1"]])
@@ -219,13 +232,14 @@ def rank_program(g, core, T, topo):
     sts = [lambda a, b, h=h: T.est[:, 4 * h + a:4 * h + b] for h in range(NH)]
     v2s, mids, sgs = [], [], []
     for h in range(NH):
-        v2s.append(update(h, (T.ones[0:1, :], T.cin[0:1, :]), lambda qd: T.dt0[0:KR, 16 * h + 4 * qd:16 * h + 4 * qd + 4],
-                          sts[h], [td0]))
+        m2 = add_moves(h, (T.ones[0:1, :], T.cin[0:1, :]), lambda qd: T.dt0[0:KR, 16 * h + 4 * qd:16 * h + 4 * qd + 4], [td0])
+        v2s.append(clamp_s(h, sts[h], m2))
     for h in range(NH):
         open_c(h)
     for h in range(NH):
         sgs.append(level(h, sts[h], v2s[h]))
-        mids.append(steps(h, sts[h], v2s[h], sgs[h][0]))
+        tq = sample_steps(h, sts[h], v2s[h])
+        mids.append((clamp_xy(h, sts[h], v2s[h]), mix(h, tq, sgs[h][0])))
     send(T.eland[:], T.est[:], "early", [mids[1][0]])
     for h in range(NH):
         offsets(h, sts[h], mids[h][0], mids[h][1], sgs[h][1])
@@ -236,7 +250,7 @@ def rank_program(g, core, T, topo):
         t = cp(T.s1[:, :, k, :], T.win[:, 0:2304], [ld1])
     ev = cp(T.win[:, 4608:9216], T.s1[:], [t])
     for h in range(NH):
-        visit(h, 0, [ld0, ld1, ea, ev])
+        moves_out(h, 0, head(h, 0, gathers(h, 0, [ld0, ld1, ea, ev])))
     for h in range(NH):
         fill(M[:, slot(h, 6) + 40:slot(h, 6) + FT], 0.0)
     fill(T.c48[0:8, 0:32], 4.0)
@@ -247,15 +261,23 @@ def rank_program(g, core, T, topo):
         prev = T.eland[:, 4 * h:4 * h + 4] if j == 0 else M[:, s + DT + 4 * j - 4:s + DT + 4 * j]
         st = lambda a, b: M[:, s + DT + 4 * j + a:s + DT + 4 * j + b]
         deps = [("arr%d_%d" % (h, j), n_in)] + ([("early", n_in)] if j == 0 else [])
-        return st, update(h, (T.ident[:], prev), lambda qd: M[0:KR, s + 4 * qd:s + 4 * qd + 4], st, deps)
+        return st, add_moves(h, (T.ident[:], prev), lambda qd: M[0:KR, s + 4 * qd:s + 4 * qd + 4], deps)
 
+    pend = None
     for j in range(NV - 1):
         for h in range(NH):
-            st, v2 = arrival(h, j)
+            st, m2 = arrival(h, j)
+            if pend:
+                m1 = head(*pend)
+            v2 = clamp_s(h, st, m2)
             tg, sg = level(h, st, v2)
-            txy, m3 = steps(h, st, v2, tg)
-            offsets(h, st, txy, m3, sg)
-            visit(h, j + 1, [])
+            tq = sample_steps(h, st, v2)
+            if pend:
+                moves_out(pend[0], pend[1], m1)
+            txy = clamp_xy(h, st, v2)
+            offsets(h, st, txy, mix(h, tq, tg), sg)
+            pend = (h, j + 1, gathers(h, j + 1, []))
+    moves_out(pend[0], pend[1], head(*pend))
 
     for h in range(NH):
         s = slot(h, NV - 1)
@@ -263,8 +285,8 @@ def rank_program(g, core, T, topo):
         if h == NH - 1:
             wait("sy", tf)
             g.sync.dma_start(T.feat[:], T.fo[:]).then_inc(T.sem.st1, 16)
-        st, v2 = arrival(h, NV - 1)
-        txy = clamp_xy(h, st, v2)
+        st, m2 = arrival(h, NV - 1)
+        txy = clamp_xy(h, st, clamp_s(h, st, m2))
         for e in range(3):
             for b in range(16):
                 th = mm(pA[h][0:8, 128 * e + b:128 * e + 112:16], T.i8[:, b:128:16], M[:, s + DT + e:s + DT + 28:4],

@@ -17,7 +17,7 @@ SCRATCH = {"s1": ("sbuf", [128, 48, 2, 48], "bfloat16"), "s2": ("sbuf", [128, 24
            "ints": ("sbuf", [128, 160], "int32")}
 for _n, _c in dict(win=18432, hd=24, h4=32, wt=256, smb=160, ident=128, iy=128, ix=128, ig=128, i8=128, ones=128, nid=8,
                    mkt=128, rep=32, sxy=64, cb1=16, cb3=32, cin=4, dt0=32, est=8, eland=8, msg=2 * (7 * WS + 2 * WL),
-                   q0=64, q1=64, tau0=32, tau1=32, ga0=128, ga1=128, gb0=128, gb1=128).items():
+                   q0=64, q1=64, tau0=32, tau1=32, ga0=128, ga1=128, gb0=128, gb1=128, hl0=28, hl1=28).items():
     SCRATCH[_n] = ("sbuf", [128, _c], "bfloat16")
 for _n, _c in dict(dio=128, dio2=128, mkc=8, mk=8, c48=48, sgc=40, sgo=16, sum0=1, sum1=1, base0=1, base1=1).items():
     SCRATCH[_n] = ("sbuf", [128, _c], "float32")
@@ -26,7 +26,7 @@ for _h in range(NH):
     for _n in "ABC":
         SCRATCH["ps%s%d" % (_n, _h)] = ("psum", [128, 512], "float32")
 
-SEMAPHORES = ["v", "a", "pe", "gp", "lds", "ld1", "ld0", "early", "loc", "st1", "st2"] + \
+SEMAPHORES = ["v", "a", "pe", "gp", "lds", "ld1", "ld0", "early", "loc", "st1", "st2", "hist0", "hist1"] + \
              ["arr%d_%d" % (h, j) for h in range(NH) for j in range(NV)]
 
 
@@ -162,10 +162,10 @@ def rank_program(g, core, T, topo):
     def open_a(h):
         mm(pA[h][0:48, 0:16], T.ones[0:96, 0:48], T.cb1[0:96, :], True, False, [last[h]["v1"]])
 
-    def add_moves(h, first, dts, deps):
+    def add_moves(h, first, dts, deps, deps2=()):
         mm(pB[h][:, 0:4], first[0], first[1], True, False, list(deps) + [last[h]["xy"]])
         for qd in range(4):
-            t = mm(pB[h][32 * qd:32 * qd + 32, 0:4], T.rep[0:KR, :], dts(qd), False, True)
+            t = mm(pB[h][32 * qd:32 * qd + 32, 0:4], T.rep[0:KR, :], dts(qd), False, True, deps2)
         return t
 
     def clamp_s(h, st, m2):
@@ -258,10 +258,15 @@ def rank_program(g, core, T, topo):
 
     def arrival(h, j):
         s = slot(h, j)
-        prev = T.eland[:, 4 * h:4 * h + 4] if j == 0 else M[:, s + DT + 4 * j - 4:s + DT + 4 * j]
+        arr = ("arr%d_%d" % (h, j), n_in)
+        if j == 0:
+            prev, known = T.eland[:, 4 * h:4 * h + 4], ("early", n_in)
+        elif j == NV - 1:
+            prev, known = T["hl%d" % h][:, 24:28], ("hist%d" % h, n_in)
+        else:
+            prev, known = M[:, s + DT + 4 * j - 4:s + DT + 4 * j], arr
         st = lambda a, b: M[:, s + DT + 4 * j + a:s + DT + 4 * j + b]
-        deps = [("arr%d_%d" % (h, j), n_in)] + ([("early", n_in)] if j == 0 else [])
-        return st, add_moves(h, (T.ident[:], prev), lambda qd: M[0:KR, s + 4 * qd:s + 4 * qd + 4], deps)
+        return st, add_moves(h, (T.ident[:], prev), lambda qd: M[0:KR, s + 4 * qd:s + 4 * qd + 4], [known], [arr])
 
     pend = None
     for j in range(NV - 1):
@@ -272,33 +277,35 @@ def rank_program(g, core, T, topo):
             v2 = clamp_s(h, st, m2)
             tg, sg = level(h, st, v2)
             tq = sample_steps(h, st, v2)
+            txy = clamp_xy(h, st, v2)
             if pend:
                 moves_out(pend[0], pend[1], m1)
-            txy = clamp_xy(h, st, v2)
             offsets(h, st, txy, mix(h, tq, tg), sg)
             pend = (h, j + 1, gathers(h, j + 1, []))
+            if j == NV - 2:
+                send(T["hl%d" % h][:], M[:, slot(h, j) + DT:slot(h, j) + DT + 28], "hist%d" % h, [last[h]["v5"]])
     moves_out(pend[0], pend[1], head(*pend))
 
     for h in range(NH):
-        s = slot(h, NV - 1)
-        tf = act(T.fo[:, :, 16 * h:16 * h + 16], M[:, s + FT:s + WL], Act.Copy, [("arr%d_%d" % (h, NV - 1), n_in)])
-        if h == NH - 1:
-            wait("sy", tf)
-            g.sync.dma_start(T.feat[:], T.fo[:]).then_inc(T.sem.st1, 16)
-        st, m2 = arrival(h, NV - 1)
-        txy = clamp_xy(h, st, clamp_s(h, st, m2))
         for e in range(3):
             for b in range(16):
-                th = mm(pA[h][0:8, 128 * e + b:128 * e + 112:16], T.i8[:, b:128:16], M[:, s + DT + e:s + DT + 28:4],
-                        True, True, [last[h]["v1"]])
-        for b in range(16):
-            tl = mm(pC[h][0:8, b:48:16], T.i8[:, b:128:16], st(0, 3), True, True, [txy])
+                th = mm(pA[h][0:8, 128 * e + b:128 * e + 112:16], T.i8[:, b:128:16], T["hl%d" % h][:, e:28:4],
+                        True, True, [last[h]["v1"], ("hist%d" % h, n_in)])
         for e in range(3):
             te = act(T.tr[0:8, e:21:3, 16 * h:16 * h + 16], pA[h][0:8, 128 * e:128 * e + 112], Act.Identity, [th],
                      bias=4.0 if e < 2 else 0.0)
-        tz = tt(T.tr[0:8, 21:24, 16 * h:16 * h + 16], pC[h][0:8, 0:48], T.c48[0:8, :], Op.add, [tl])
     wait("sy", te)
     g.sync.dma_start(T.trail[:, 0:672], T.tr[0:8, 0:21, :]).then_inc(T.sem.st1, 16)
+    for h in range(NH):
+        s = slot(h, NV - 1)
+        tf = act(T.fo[:, :, 16 * h:16 * h + 16], M[:, s + FT:s + WL], Act.Copy, [("arr%d_%d" % (h, NV - 1), n_in)])
+        st, m2 = arrival(h, NV - 1)
+        txy = clamp_xy(h, st, clamp_s(h, st, m2))
+        for b in range(16):
+            tl = mm(pC[h][0:8, b:48:16], T.i8[:, b:128:16], st(0, 3), True, True, [txy])
+        tz = tt(T.tr[0:8, 21:24, 16 * h:16 * h + 16], pC[h][0:8, 0:48], T.c48[0:8, :], Op.add, [tl])
+    wait("sy", tf)
+    g.sync.dma_start(T.feat[:], T.fo[:]).then_inc(T.sem.st1, 16)
     wait("a", tz)
     g.scalar.dma_start(T.trail[:, 672:768], T.tr[0:8, 21:24, :]).then_inc(T.sem.st2, 16)
     wait("gp", ("loc", cnt["loc"]), ("v", cnt["v"]), ("a", cnt["a"]), ("pe", cnt["pe"]), ("gp", cnt["gp"]),

@@ -2,31 +2,33 @@ from concourse.mybir import AluOpType as Op, ActivationFunctionType as Act
 
 NH = 2
 NV = 8
-WS, WL = 48, 176
-DT, FT = 16, 48
-KR = 65
+L = 12
+DT = 4 * L
+WS = DT + 32
+BIG = 1024
+INTER = (0, 1)
 
 
 def slot(h, j):
-    per = 7 * WS + 2 * WL
-    return h * per + ((j + 1) * WS if j <= 6 else 7 * WS + WL)
+    return h * DT if j < 0 else NH * DT + (h * NV + j) * WS
 
 
 SCRATCH = {"s1": ("sbuf", [128, 48, 2, 48], "bfloat16"), "s2": ("sbuf", [128, 24, 4, 24], "bfloat16"),
            "fo": ("sbuf", [128, 8, 32], "bfloat16"), "tr": ("sbuf", [128, 24, 32], "float32"),
            "ints": ("sbuf", [128, 160], "int32")}
-for _n, _c in dict(win=18432, hd=24, h4=32, wt=256, smb=160, ident=128, iy=128, ix=128, ig=128, i8=128, ones=128, nid=8,
-                   mkt=128, rep=32, sxy=64, cb1=16, cb3=32, cin=4, dt0=32, est=8, eland=8, msg=2 * (7 * WS + 2 * WL),
-                   q0=64, q1=64, tau0=32, tau1=32, ga0=128, ga1=128, gb0=128, gb1=128, hl0=28, hl1=28).items():
+for _n, _c in dict(win=18432, hd=24, h4=32, wt=256, smb=176, ident=128, iy=128, ix=128, ones=128,
+                   mkt=128, rep=32, rep4=32, sxy=64, ca=DT, cb=L, cc=32, cd=2, ct=48, est=8, eland=8, fland=256,
+                   msg=NH * (DT + NV * WS), seg=256, q0=64, q1=64, lo=NH * DT, ga0=512, ga1=512, gb0=512, gb1=512,
+                   hl0=28, hl1=28).items():
     SCRATCH[_n] = ("sbuf", [128, _c], "bfloat16")
-for _n, _c in dict(dio=128, dio2=128, mkc=8, mk=8, c48=48, sgc=40, sgo=16, sum0=1, sum1=1, base0=1, base1=1).items():
+for _n, _c in dict(dio=128, dio2=128, mkc=8, mk=8, f0=1, f1=1, base0=1, base1=1).items():
     SCRATCH[_n] = ("sbuf", [128, _c], "float32")
 for _h in range(NH):
     SCRATCH["off%d" % _h] = ("sbuf", [128, 32], "uint16")
-    for _n in "ABC":
+    for _n in "ABCD":
         SCRATCH["ps%s%d" % (_n, _h)] = ("psum", [128, 512], "float32")
 
-SEMAPHORES = ["v", "a", "pe", "gp", "lds", "ld1", "ld0", "early", "loc", "st1", "st2", "hist0", "hist1"] + \
+SEMAPHORES = ["v", "a", "pe", "gp", "lds", "ld1", "ld0", "early", "loc", "st1", "st2", "hist0", "hist1", "fin"] + \
              ["arr%d_%d" % (h, j) for h in range(NH) for j in range(NV)]
 
 
@@ -69,6 +71,10 @@ def rank_program(g, core, T, topo):
         wait("v", *deps)
         return done("v", g.vector.tensor_copy(out, a))
 
+    def scan(out, a, b, op0, op1, deps=()):
+        wait("v", *deps)
+        return done("v", g.vector.tensor_tensor_scan(out, a, b, 0.0, op0, op1))
+
     def fill(ap, c, deps=()):
         wait("v", *deps)
         return done("v", g.vector.memset(ap, c))
@@ -81,15 +87,16 @@ def rank_program(g, core, T, topo):
         wait("a", *deps)
         return done("a", g.scalar.activation(out, in_, func, **kw))
 
+    def const(ap, cols, c):
+        return done("gp", g.iota(ap, [[0, cols]], c, 0, allow_small_or_imprecise_dtypes=True))
+
     def send(dst, src, sem, deps):
         wait("gp", *deps)
         g.remote_dma(dst, src, T.sem[sem], T.sem.loc, pid, rid, mask)
         cnt["loc"] += n_out
 
     M = T.msg
-    pA = [T["psA%d" % h] for h in range(NH)]
-    pB = [T["psB%d" % h] for h in range(NH)]
-    pC = [T["psC%d" % h] for h in range(NH)]
+    pA, pB, pC, pD = ([T["ps%s%d" % (b, h)] for h in range(NH)] for b in "ABCD")
 
     g.scalar.dma_start(T.ints[0:8, 64:160], T.box[:]).then_inc(T.sem.lds, 16)
     g.scalar.dma_start(T.ints[0:8, 0:32], T.sy[:]).then_inc(T.sem.lds, 16)
@@ -101,211 +108,245 @@ def rank_program(g, core, T, topo):
 
     io1 = done("gp", g.iota(T.dio[:], [[-1, 128]], 0, 1, allow_small_or_imprecise_dtypes=True))
     io2 = done("gp", g.iota(T.dio2[0:8, :], [[1, 8], [0, 16]], 0, -1, allow_small_or_imprecise_dtypes=True))
-    fill(T.ones[:], 1.0)
+    for c, val in enumerate((144, 156, BIG, 144, 156, BIG, 0, 12, 216, BIG, BIG, 152)):
+        tca = const(T.ca[0:32, c:DT:L], 4, val)
+    for c, val in enumerate((BIG, 132, -BIG, BIG, 132, -BIG, BIG, None, 132, 139, 140, 151)):
+        if val is not None:
+            tlo = const(T.lo[0:48, c:NH * DT:L], 4 * NH, val)
+    fill(T.ones[:], 1.0 / 32)
     fill(T.rep[0:64, :], 0.0)
-    fill(T.rep[64:KR, :], -1.0)
-    fill(T.dt0[0:KR, :], 0.0)
-    fill(T.cb1[0:32, :], 0.75)
-    fill(T.cb1[32:64, :], -2.0 ** -9)
-    fill(T.cb1[64:96, :], 2.0 ** -18)
+    fill(M[:, 0:NH * DT], 0.0)
+    fill(T.smb[0:8, 160:176], 0.0)
+    fill(T.cb[0:64, :], 0.0)
+    fill(T.ca[32:64, :], 0.0)
+    fill(T.seg[:], 1.0)
+    fill(T.win[:, 4584:4608], 0.0)
+    fill(T.cc[0:32, :], 39936.0)
+    fill(T.cc[32:64, :], -68.0)
+    fill(T.cc[64:96, :], -0.25)
+    fill(T.cd[0:32, :], -38.25)
     tid = ts(T.ident[:], T.dio[:], 0.0, None, Op.is_equal, deps=[io1])
     t = ts(T.mkc[:], T.dio[:, 0:128:16], 0.0, 15.0, Op.max, Op.min)
-    ts(T.nid[0:8, :], T.dio[0:8, 0:8], 0.0, -1.0, Op.is_equal, Op.mult)
     ts(T.mkt[0:8, :], T.dio2[0:8, :], 0.0, None, Op.is_equal, deps=[io2])
     tmk = tt(T.mk[:], T.mkc[:], T.dio[:, 0:128:16], Op.is_equal, [t])
     cp(T.rep[0:16, 0:16], T.ident[0:16, 0:16])
-    cp(T.rep[32:48, 16:32], T.ident[32:48, 32:48])
-    fill(T.cb1[32:64, 3:16:4], 2.0 ** -9)
-    fill(T.cb1[64:96, 3:16:4], -2.0 ** -18)
-    fill(T.cb3[0:32, :], 12.5)
-    fill(T.cb3[32:64, :], 7.0 / 2048)
-    fill(T.cin[0:1, 0:2], -0.5)
-    fill(T.cin[0:1, 2:3], 0.0)
-    fill(T.cin[0:1, 3:4], 11.5)
-    fill(T.sgc[:, 0:33], -23.5 / 8)
-    fill(T.sgc[:, 33:35], -11.5 / 8)
-    fill(T.sgc[:, 35:40], -1000.0)
-    for h in range(NH):
-        fill(M[:, slot(h, -1):slot(h, -1) + DT], 24.0)
-    for buf, c in ((T.iy, -12.0), (T.ix, -0.125), (T.ig, 5.0 / 64), (T.i8, 8.0)):
+    t = cp(T.rep[32:48, 16:32], T.ident[32:48, 32:48])
+    fill(T.cb[0:32, 2:6:3], -144.0)
+    fill(T.cb[0:32, 8:9], -128.0)
+    fill(T.cb[0:32, 9:10], -1.0)
+    fill(T.cb[0:32, 11:12], 69.0)
+    fill(T.cb[32:64, 11:12], 15.0 / 32)
+    trep = act(T.rep4[0:48, :], T.rep[0:48, :], Act.Copy, [t], scale=0.25)
+    for buf, c in ((T.iy, -96.0), (T.ix, -1.0)):
         tis = act(buf[:], T.ident[:], Act.Copy, [tid], scale=c)
 
-    tb = ts(T.smb[0:8, 64:160], T.ints[0:8, 64:160], 0.125, None, Op.mult, deps=[lds])
-    tsx = ts(T.smb[0:8, 0:64], T.ints[0:8, 0:64], 0.5, None, Op.mult)
+    ts(T.smb[0:8, 64:128], T.ints[0:8, 64:128], -1.0, 240.0, Op.mult, Op.add, deps=[lds])
+    tb = ts(T.smb[0:8, 128:160], T.ints[0:8, 128:160], 128.0, None, Op.add)
+    tsx = ts(T.smb[0:8, 0:64], T.ints[0:8, 0:64], -1.0 / 16, None, Op.mult)
     for h in range(NH):
         for e in range(4):
             for blk in range(2):
-                c0 = 64 + 32 * min(e, 2) + 16 * h
-                src = T.nid if e == 3 else T.ident
-                tm0 = mm(pA[0][32 * blk:32 * blk + 16, 16 * h + e:16 * h + 16:4], T.smb[0:8, c0:c0 + 16],
-                         src[0:8, blk:8:2], True, True, [tb])
+                c0, wd = 64 + 32 * min(e, 2) + 16 * h, 32 - 16 * blk
+                tm0 = mm(pA[0][32 * blk:32 * blk + wd, 16 * h + e:16 * h + 16:4], T.smb[0:8, c0:c0 + wd],
+                         T.ident[0:8, blk:8:2], True, True, [tb])
     for tbl in range(2):
         for s in range(4):
             for kk in range(2):
                 c0 = 32 * tbl + 8 * s + 4 * kk
                 tm1 = mm(pC[1][:, c0:c0 + 4], T.mkt[0:8, :], T.smb[0:8, 32 * tbl + 2 * s + kk:32 * tbl + 32:8],
                          True, True, [tsx])
-    act(T.h4[:, 0:24], T.hd[:], Act.Copy, [lds], scale=1.0 / 4096)
-    t = act(T.h4[:, 24:32], T.hd[:, 16:24], Act.Copy, scale=-1.0 / 4096)
+    for c, sign in ((0, 1), (3, 1), (6, -1)):
+        fill(T.ca[32:64, c:DT:L], sign * 33.0 / 64)
+    fill(T.seg[:, 0:256:4], 0.0)
+    t = cp(M[0:48, 2:NH * DT:3], pA[0][0:48, 0:32], [tm0])
+    ts(M[0:48, 9:NH * DT:L], pA[0][0:48, 2:32:4], 139.0, None, Op.max)
+    ts(M[0:48, 10:NH * DT:L], pA[0][0:48, 2:32:4], 140.0, None, Op.max)
+    cp(T.sxy[:], pC[1][:, 0:64], [tm1])
+    tsxy = td0 = ts(M[0:48, 11:NH * DT:L], pA[0][0:48, 2:32:4], 151.0, 152.0, Op.max, Op.min, deps=[t])
+    act(T.h4[:, 0:16], T.hd[:, 0:16], Act.Copy, [lds], scale=-1.0 / 512)
+    act(T.h4[:, 16:24], T.hd[:, 16:24], Act.Copy, scale=1.0 / 512)
+    t = act(T.h4[:, 24:32], T.hd[:, 16:24], Act.Copy, scale=0.0)
     for gi in range(8):
         c0 = 128 * (gi % 2) + 32 * (gi // 2)
-        act(T.wt[:, c0:c0 + 32], T.h4[:], Act.Identity, [t, tmk], scale=T.mk[:, gi:gi + 1])
-    cp(T.dt0[0:16, :], pA[0][0:16, 0:32], [tm0])
-    td0 = cp(T.dt0[32:48, :], pA[0][32:48, 0:32])
-    tsxy = cp(T.sxy[:], pC[1][:, 0:64], [tm1])
+        twt = act(T.wt[:, c0:c0 + 32], T.h4[:], Act.Identity, [t, tmk], scale=T.mk[:, gi:gi + 1])
 
-    last = [{"v1": td0, "v5": tsxy, "xy": None} for _ in range(NH)]
+    last = [{"upd": tsxy, "off": tsxy, "lev": tsxy} for _ in range(NH)]
 
-    def open_c(h):
-        mm(pC[h][:, 0:32], T.ones[0:64, :], T.cb3[0:64, :], True, False, [last[h]["v5"]])
+    def open_state(h, level=True):
+        mm(pB[h][:, 0:L], T.ones[0:64, :], T.cb[0:64, :], True, False, [last[h]["lev"]])
+        if level:
+            mm(pD[h][:, 0:1], T.ones[0:32, :], T.cd[0:32, 0:1], True, False)
 
-    def open_a(h):
-        mm(pA[h][0:48, 0:16], T.ones[0:96, 0:48], T.cb1[0:96, :], True, False, [last[h]["v1"]])
+    def open_offsets(h):
+        mm(pC[h][:, 0:32], T.ones[0:96, :], T.cc[0:96, :], True, False, [last[h]["off"]])
 
-    def add_moves(h, first, dts, deps, deps2=()):
-        mm(pB[h][:, 0:4], first[0], first[1], True, False, list(deps) + [last[h]["xy"]])
+    def turn(h, s, prev, deps, level=True):
+        if prev is not None:
+            mm(pB[h][:, 2:6:3], T.ident[:], prev, False, False, deps)
         for qd in range(4):
-            t = mm(pB[h][32 * qd:32 * qd + 32, 0:4], T.rep[0:KR, :], dts(qd), False, True, deps2)
-        return t
+            tb_ = mm(pB[h][32 * qd:32 * qd + 32, 0:L], T.rep[0:48, :], M[0:48, s + L * qd:s + L * qd + L], False, True, deps)
+        td = None
+        for qd in range(4 if level else 0):
+            td = mm(pD[h][32 * qd:32 * qd + 32, 0:1], T.rep4[0:48, :], M[0:48, s + L * qd + 11:s + L * qd + 12], False, True,
+                    [trep])
+        return tb_, td
 
-    def clamp_s(h, st, m2):
-        return ts(st(2, 4), pB[h][:, 2:4], 0.5, 11.0, Op.max, Op.min, deps=[m2])
+    def clamp(h, st, tb_):
+        return ts(st(0, 4), pB[h][:, 2:L:3], pB[h][:, 8:9], 96.0, Op.max, Op.min, deps=[tb_])
 
-    def clamp_xy(h, st, v2):
-        last[h]["xy"] = ts(st(0, 2), pB[h][:, 0:2], -0.5, st(3, 4), Op.max, Op.min, deps=[v2])
-        return last[h]["xy"]
+    def begin(h, st, tn):
+        tq = ts(T["q%d" % h][:], T.sxy[:], pB[h][:, 8:9], pB[h][:, 11:12], Op.mult, Op.add, deps=[tn[0], tsxy])
+        txy = clamp(h, st, tn[0])
+        last[h]["lev"] = ts(T["f%d" % h][:], pB[h][:, 9:10], pB[h][:, 10:11], pD[h][:, 0:1], Op.subtract, Op.mult,
+                            deps=[tn[1]])
+        return tq, txy
 
-    def level(h, st, v2):
-        tg = act(T["tau%d" % h][:], T.sgc[:, 0:32], Act.Sign, [v2], bias=st(2, 3))
-        return tg, act(T.sgo[:, 8 * h:8 * h + 8], T.sgc[:, 32:40], Act.Sign, bias=st(2, 3),
-                       accum_out=T["sum%d" % h][:])
-
-    def sample_steps(h, st, v2):
-        return ts(T["q%d" % h][:], T.sxy[:], st(2, 3), 131.53125, Op.mult, Op.add, deps=[v2])
-
-    def mix(h, tq, tg):
+    def mix(h, tq):
         qb = T["q%d" % h]
         mm(pC[h][:, 0:32], T.iy[:], qb[:, 0:32], False, False, [tq, tis])
-        mm(pC[h][:, 0:32], T.ix[:], qb[:, 32:64], False, False)
-        return mm(pC[h][:, 0:32], T.ig[:], T["tau%d" % h][:], False, True, [tg])
+        return mm(pC[h][:, 0:32], T.ix[:], qb[:, 32:64], False, True)
 
-    def offsets(h, st, txy, m3, sg):
-        bs = T["base%d" % h]
-        v4 = ts(bs[:], st(1, 2), -96.0, st(0, 1), Op.mult, Op.subtract, deps=[txy])
-        last[h]["v5"] = ts(T["off%d" % h][:], pC[h][:, 0:32], bs[:], T["sum%d" % h][:], Op.add, Op.mult,
-                           deps=[v4, m3, sg])
+    def corner(h, st, txy):
+        return ts(T["base%d" % h][:], st(1, 2), -96.0, st(0, 1), Op.mult, Op.subtract, deps=[txy])
 
-    def feats(h, j):
-        return (M, slot(h, j - 1) + FT) if j == NV - 1 else (T["gb%d" % h], 0)
+    def offsets(h, tc, m3):
+        last[h]["off"] = ts(T["off%d" % h][:], pC[h][:, 0:32], T["base%d" % h][:], T["f%d" % h][:], Op.add, Op.mult,
+                            deps=[tc, m3])
 
-    def gathers(h, j, ready):
-        off, ga, gb = T["off%d" % h], T["ga%d" % h], T["gb%d" % h]
-        deps = [last[h]["v5"]] + ready
-        open_a(h)
-        if j < NV - 1:
-            open_c(h)
-        fb, f0 = feats(h, j)
-        ta = act(ga[:, 0:64], T.win[:].indirect(off[:, 0:4]), Act.Copy, deps)
-        tk = [ta, cp(ga[:, 64:128], T.win[:].indirect(off[:, 4:8]), deps)]
-        for s, (src, dst, d0) in enumerate(((ga, gb, 0), (gb, ga, 0), (ga, fb, f0))):
-            for k in (1, 0):
-                c = 8 * s + 8 + 4 * k
-                tk[k] = tt(dst[:, d0 + 64 * k:d0 + 64 * k + 64], T.win[:].indirect(off[:, c:c + 4]),
-                           src[:, 64 * k:64 * k + 64], Op.max, [tk[k]])
+    def bounds(h, s, deps):
+        act(T.lo[0:48, DT * h + 7:DT * h + DT:L], M[0:48, s + 8:s + DT:L], Act.Identity,
+            list(deps) + [last[h]["upd"]], bias=-12.0)
+
+    def open_head(h, s):
+        mm(pA[h][0:48, 0:DT], T.ones[0:63, 0:48], T.ca[0:63, :], True, False, [last[h]["upd"], tca])
+        for c in (6, 7):
+            mm(pA[h][0:48, c:DT:L], T.ident[0:48, 0:48], M[0:48, s + 8:s + DT:L], False, False)
+
+    def gathers(h, ready):
+        off, ga = T["off%d" % h], T["ga%d" % h]
+        deps = [last[h]["off"]] + ready
+        for s in (0, 1):
+            ta = act(ga[:, s:512:4], T.win[:].indirect(off[:, 8 * s:8 * s + 8]), Act.Copy, deps)
+        for s in (2, 3):
+            tv = cp(ga[:, s:512:4], T.win[:].indirect(off[:, 8 * s:8 * s + 8]), deps)
+        return ta, tv
+
+    def pool(h, tg):
+        ga, gb = T["ga%d" % h], T["gb%d" % h]
+        tk = [None, None]
+        for k in (1, 0):
+            tk[k] = scan(gb[:, 256 * k:256 * k + 256], T.seg[:], ga[:, 256 * k:256 * k + 256], Op.mult, Op.max, tg)
         return tk
 
-    def head(h, j, tk):
-        fb, f0 = feats(h, j)
+    def head(h, tk):
+        gb = T["gb%d" % h]
         for b in range(7, -1, -1):
             for blk in range(2):
-                wd = 32 if b == 0 and blk == 0 else 16
-                m1 = mm(pA[h][32 * blk:32 * blk + wd, 0:16], fb[:, f0 + 16 * b:f0 + 16 * b + wd],
-                        T.wt[:, 128 * blk + b:128 * blk + 128:8], False, b == 0, [tk[b // 4]])
+                wd = 128 if b == 0 and blk == 0 else 64
+                m1 = mm(pA[h][32 * blk:32 * blk + wd // 4, 0:DT:3], gb[:, 64 * b + 3:64 * b + wd:4],
+                        T.wt[:, 128 * blk + b:128 * blk + 128:8], False, b == 0, [tk[b // 4], twt])
         return m1
 
-    def moves_out(h, j, m1):
+    def update(h, j, m1):
         s0 = slot(h, j - 1)
-        last[h]["v1"] = ts(M[0:48, s0:s0 + DT], pA[h][0:48, 0:16], 22.5, 25.5, Op.max, Op.min, deps=[m1])
-        w = WL if j == NV - 1 else DT + 4 * j
-        send(M[:, slot(h, j):slot(h, j) + w], M[:, s0:s0 + w], "arr%d_%d" % (h, j), [last[h]["v1"]])
+        last[h]["upd"] = scan(M[0:48, s0:s0 + DT], T.lo[0:48, DT * h:DT * h + DT], pA[h][0:48, 0:DT], Op.max, Op.min,
+                              [m1, tlo])
+        w = DT if j == NV - 1 else DT + 4 * j
+        send(M[:, slot(h, j):slot(h, j) + w], M[:, s0:s0 + w], "arr%d_%d" % (h, j), [last[h]["upd"]])
 
     sts = [lambda a, b, h=h: T.est[:, 4 * h + a:4 * h + b] for h in range(NH)]
-    v2s, mids, sgs = [], [], []
+    mids = []
     for h in range(NH):
-        m2 = add_moves(h, (T.ones[0:1, :], T.cin[0:1, :]), lambda qd: T.dt0[0:KR, 16 * h + 4 * qd:16 * h + 4 * qd + 4], [td0])
-        v2s.append(clamp_s(h, sts[h], m2))
+        open_state(h)
+        open_offsets(h)
+    tns = [turn(h, slot(h, -1), None, [td0]) for h in range(NH)]
     for h in range(NH):
-        open_c(h)
+        mids.append(begin(h, sts[h], tns[h]))
+        bounds(h, slot(h, -1), [td0])
+    send(T.eland[:], T.est[:], "early", [mids[1][1]])
     for h in range(NH):
-        sgs.append(level(h, sts[h], v2s[h]))
-        tq = sample_steps(h, sts[h], v2s[h])
-        mids.append((clamp_xy(h, sts[h], v2s[h]), mix(h, tq, sgs[h][0])))
-    send(T.eland[:], T.est[:], "early", [mids[1][0]])
+        offsets(h, corner(h, sts[h], mids[h][1]), mix(h, mids[h][0]))
     for h in range(NH):
-        offsets(h, sts[h], mids[h][0], mids[h][1], sgs[h][1])
+        open_head(h, slot(h, -1))
+        open_state(h)
+        open_offsets(h)
     for k in range(4):
         t = act(T.s2[:, :, k, :], T.win[:, 2304:2880], Act.Copy, [ld1])
-    ea = act(T.win[:, 2304:4608], T.s2[:], Act.Copy, [t])
     for k in range(2):
-        t = cp(T.s1[:, :, k, :], T.win[:, 0:2304], [ld1])
-    ev = cp(T.win[:, 4608:9216], T.s1[:], [t])
-    for h in range(NH):
-        moves_out(h, 0, head(h, 0, gathers(h, 0, [ld0, ld1, ea, ev])))
-    for h in range(NH):
-        fill(M[:, slot(h, 6) + 40:slot(h, 6) + FT], 0.0)
-    fill(T.c48[0:8, 0:32], 4.0)
-    fill(T.c48[0:8, 32:48], 0.0)
+        tv = cp(T.s1[:, :, k, :], T.win[:, 0:2304], [ld1])
+    ea = act(T.win[:, 2280:4584], T.s2[:], Act.Copy, [t, tv])
+    ev = cp(T.win[:, 4608:9216], T.s1[:], [tv])
+    tg0 = gathers(0, [ld0, ld1, ea, ev])
+    tk0 = pool(0, tg0)
+    tg1 = gathers(1, [])
+    update(0, 0, head(0, tk0))
+    pend = (1, 0, pool(1, tg1))
 
-    def arrival(h, j):
+    def arrival(h, j, level=True):
         s = slot(h, j)
         arr = ("arr%d_%d" % (h, j), n_in)
         if j == 0:
-            prev, known = T.eland[:, 4 * h:4 * h + 4], ("early", n_in)
+            prev, known = T.eland[:, 4 * h:4 * h + 2], ("early", n_in)
         elif j == NV - 1:
-            prev, known = T["hl%d" % h][:, 24:28], ("hist%d" % h, n_in)
+            prev, known = T["hl%d" % h][:, 24:26], ("hist%d" % h, n_in)
         else:
-            prev, known = M[:, s + DT + 4 * j - 4:s + DT + 4 * j], arr
+            prev, known = M[:, s + DT + 4 * j - 4:s + DT + 4 * j - 2], arr
         st = lambda a, b: M[:, s + DT + 4 * j + a:s + DT + 4 * j + b]
-        return st, add_moves(h, (T.ident[:], prev), lambda qd: M[0:KR, s + 4 * qd:s + 4 * qd + 4], [known], [arr])
+        if level:
+            bounds(h, s, [arr])
+        return st, turn(h, s, prev, [known, arr], level)
 
-    pend = None
+    def keep_feats(h, tk):
+        return act(T.fo[:, :, 16 * h:16 * h + 16], T["gb%d" % h][:, 3:512:4], Act.Copy, [tk[0]])
+
     for j in range(NV - 1):
         for h in range(NH):
-            st, m2 = arrival(h, j)
-            if pend:
-                m1 = head(*pend)
-            v2 = clamp_s(h, st, m2)
-            tg, sg = level(h, st, v2)
-            tq = sample_steps(h, st, v2)
-            txy = clamp_xy(h, st, v2)
-            if pend:
-                moves_out(pend[0], pend[1], m1)
-            offsets(h, st, txy, mix(h, tq, tg), sg)
-            pend = (h, j + 1, gathers(h, j + 1, []))
+            if not INTER[h]:
+                m1 = head(pend[0], pend[2])
+            st, tn = arrival(h, j)
+            if INTER[h]:
+                m1 = head(pend[0], pend[2])
+            else:
+                update(pend[0], pend[1], m1)
+            tq, txy = begin(h, st, tn)
+            m3 = mix(h, tq)
+            tc = corner(h, st, txy)
+            if INTER[h]:
+                update(pend[0], pend[1], m1)
+            offsets(h, tc, m3)
+            open_head(h, slot(h, j))
+            open_state(h, j < NV - 2)
+            if j < NV - 2:
+                open_offsets(h)
+            pend = (h, j + 1, pool(h, gathers(h, [])))
             if j == NV - 2:
-                send(T["hl%d" % h][:], M[:, slot(h, j) + DT:slot(h, j) + DT + 28], "hist%d" % h, [last[h]["v5"]])
-    moves_out(pend[0], pend[1], head(*pend))
+                send(T["hl%d" % h][:], M[:, slot(h, j) + DT:slot(h, j) + DT + 28], "hist%d" % h, [last[h]["off"]])
+                tf = keep_feats(h, pend[2])
+    update(pend[0], pend[1], head(pend[0], pend[2]))
+    send(T.fland[:], T.fo[:], "fin", [tf])
 
+    fill(T.ct[0:32, 0:32], -96.0)
+    tct = fill(T.ct[0:32, 32:48], 0.0)
     for h in range(NH):
         for e in range(3):
             for b in range(16):
-                th = mm(pA[h][0:8, 128 * e + b:128 * e + 112:16], T.i8[:, b:128:16], T["hl%d" % h][:, e:28:4],
-                        True, True, [last[h]["v1"], ("hist%d" % h, n_in)])
+                th = mm(pA[h][0:8, 128 * e + b:128 * e + 112:16], T.ident[:, b:128:16], T["hl%d" % h][:, e:28:4],
+                        True, True, [last[h]["upd"], ("hist%d" % h, n_in)])
         for e in range(3):
             te = act(T.tr[0:8, e:21:3, 16 * h:16 * h + 16], pA[h][0:8, 128 * e:128 * e + 112], Act.Identity, [th],
-                     bias=4.0 if e < 2 else 0.0)
+                     bias=96.0 if e < 2 else 0.0, scale=-1.0 if e < 2 else 1.0)
     wait("sy", te)
     g.sync.dma_start(T.trail[:, 0:672], T.tr[0:8, 0:21, :]).then_inc(T.sem.st1, 16)
     for h in range(NH):
-        s = slot(h, NV - 1)
-        tf = act(T.fo[:, :, 16 * h:16 * h + 16], M[:, s + FT:s + WL], Act.Copy, [("arr%d_%d" % (h, NV - 1), n_in)])
-        st, m2 = arrival(h, NV - 1)
-        txy = clamp_xy(h, st, clamp_s(h, st, m2))
+        mm(pC[h][0:8, 0:48], T.ones[0:32, 0:8], T.ct[0:32, :], True, False, [tct])
+    for h in range(NH):
+        st, tn = arrival(h, NV - 1, False)
+        txy = clamp(h, st, tn[0])
         for b in range(16):
-            tl = mm(pC[h][0:8, b:48:16], T.i8[:, b:128:16], st(0, 3), True, True, [txy])
-        tz = tt(T.tr[0:8, 21:24, 16 * h:16 * h + 16], pC[h][0:8, 0:48], T.c48[0:8, :], Op.add, [tl])
-    wait("sy", tf)
-    g.sync.dma_start(T.feat[:], T.fo[:]).then_inc(T.sem.st1, 16)
+            tl = mm(pC[h][0:8, b:48:16], T.ident[:, b:128:16], st(0, 3), False, b == 15, [txy])
+        tz = act(T.tr[0:8, 21:24, 16 * h:16 * h + 16], pC[h][0:8, 0:48], Act.Abs, [tl])
+    wait("sy", ("fin", n_in))
+    g.sync.dma_start(T.feat[:], T.fland[:]).then_inc(T.sem.st1, 16)
     wait("a", tz)
     g.scalar.dma_start(T.trail[:, 672:768], T.tr[0:8, 21:24, :]).then_inc(T.sem.st2, 16)
     wait("gp", ("loc", cnt["loc"]), ("v", cnt["v"]), ("a", cnt["a"]), ("pe", cnt["pe"]), ("gp", cnt["gp"]),

@@ -5,6 +5,7 @@ NV = 8
 L = 12
 DT = 4 * L
 WS = DT + 32
+RV = 36
 BIG = 1024
 INTER = (0, 1)
 
@@ -13,10 +14,10 @@ def slot(h, j):
     return h * DT if j < 0 else NH * DT + (h * NV + j) * WS
 
 
-SCRATCH = {"s1": ("sbuf", [128, 48, 2, 48], "bfloat16"), "s2": ("sbuf", [128, 24, 4, 24], "bfloat16"),
+SCRATCH = {"s1": ("sbuf", [128, RV, 2, 48], "bfloat16"),
            "fo": ("sbuf", [128, 8, 32], "bfloat16"), "tr": ("sbuf", [128, 24, 32], "float32"),
            "ints": ("sbuf", [128, 160], "int32")}
-for _n, _c in dict(win=18432, hd=24, h4=32, wt=256, smb=176, ident=128, iy=128, ix=128, ones=128,
+for _n, _c in dict(win=18432, raw=2880, hd=24, h4=32, wt=256, smb=176, ident=128, iy=128, ix=128, ones=128,
                    mkt=128, rep=32, rep4=32, sxy=64, ca=DT, cb=L, cc=32, cd=2, ct=48, est=8, eland=8, fland=256,
                    msg=NH * (DT + NV * WS), seg=256, q0=64, q1=64, lo=NH * DT, ga0=512, ga1=512, gb0=512, gb1=512,
                    hl0=28, hl1=28).items():
@@ -26,9 +27,9 @@ for _n, _c in dict(dio=128, dio2=128, mkc=8, mk=8, f0=1, f1=1, base0=1, base1=1)
 for _h in range(NH):
     SCRATCH["off%d" % _h] = ("sbuf", [128, 32], "uint16")
     for _n in "ABCD":
-        SCRATCH["ps%s%d" % (_n, _h)] = ("psum", [128, 512], "float32")
+        SCRATCH["ps%s%d" % (_n, _h)] = ("psum", [128, 4, 128] if _n in "AD" else [128, 512], "float32")
 
-SEMAPHORES = ["v", "a", "pe", "gp", "lds", "ld1", "ld0", "early", "loc", "st1", "st2", "hist0", "hist1", "fin"] + \
+SEMAPHORES = ["v", "a", "pe", "gp", "lds", "ldh", "ld1", "ld0", "early", "loc", "st1", "st2", "hist0", "hist1", "fin"] + \
              ["arr%d_%d" % (h, j) for h in range(NH) for j in range(NV)]
 
 
@@ -100,11 +101,11 @@ def rank_program(g, core, T, topo):
 
     g.scalar.dma_start(T.ints[0:8, 64:160], T.box[:]).then_inc(T.sem.lds, 16)
     g.scalar.dma_start(T.ints[0:8, 0:32], T.sy[:]).then_inc(T.sem.lds, 16)
-    g.sync.dma_start(T.hd[:], T.head[:]).then_inc(T.sem.lds, 16)
     g.sync.dma_start(T.ints[0:8, 32:64], T.sx[:]).then_inc(T.sem.lds, 16)
-    g.sync.dma_start(T.win[:, 0:2880], T.pyr[:, 9216:12096]).then_inc(T.sem.ld1, 16)
+    g.sync.dma_start(T.hd[:], T.head[:]).then_inc(T.sem.ldh, 16)
+    g.sync.dma_start(T.raw[:], T.pyr[:, 9216:12096]).then_inc(T.sem.ld1, 16)
     g.sync.dma_start(T.win[:, 9216:18432], T.pyr[:, 0:9216]).then_inc(T.sem.ld0, 16)
-    lds, ld1, ld0 = ("lds", 64), ("ld1", 16), ("ld0", 16)
+    lds, ldh, ld1, ld0 = ("lds", 48), ("ldh", 16), ("ld1", 16), ("ld0", 16)
 
     io1 = done("gp", g.iota(T.dio[:], [[-1, 128]], 0, 1, allow_small_or_imprecise_dtypes=True))
     io2 = done("gp", g.iota(T.dio2[0:8, :], [[1, 8], [0, 16]], 0, -1, allow_small_or_imprecise_dtypes=True))
@@ -120,34 +121,33 @@ def rank_program(g, core, T, topo):
     fill(T.cb[0:64, :], 0.0)
     fill(T.ca[32:64, :], 0.0)
     fill(T.seg[:], 1.0)
-    fill(T.win[:, 4584:4608], 0.0)
-    fill(T.cc[0:32, :], 39936.0)
-    fill(T.cc[32:64, :], -68.0)
-    fill(T.cc[64:96, :], -0.25)
-    fill(T.cd[0:32, :], -38.25)
     tid = ts(T.ident[:], T.dio[:], 0.0, None, Op.is_equal, deps=[io1])
     t = ts(T.mkc[:], T.dio[:, 0:128:16], 0.0, 15.0, Op.max, Op.min)
-    ts(T.mkt[0:8, :], T.dio2[0:8, :], 0.0, None, Op.is_equal, deps=[io2])
+    fill(T.cc[0:32, :], 39936.0)
+    fill(T.cc[32:64, :], -68.0)
     tmk = tt(T.mk[:], T.mkc[:], T.dio[:, 0:128:16], Op.is_equal, [t])
     cp(T.rep[0:16, 0:16], T.ident[0:16, 0:16])
     t = cp(T.rep[32:48, 16:32], T.ident[32:48, 32:48])
+    ts(T.mkt[0:8, :], T.dio2[0:8, :], 0.0, None, Op.is_equal, deps=[io2])
+    fill(T.cc[64:96, :], -0.25)
+    fill(T.cd[0:32, :], -38.25)
     fill(T.cb[0:32, 2:6:3], -144.0)
-    fill(T.cb[0:32, 8:9], -128.0)
-    fill(T.cb[0:32, 9:10], -1.0)
-    fill(T.cb[0:32, 11:12], 69.0)
-    fill(T.cb[32:64, 11:12], 15.0 / 32)
-    trep = act(T.rep4[0:48, :], T.rep[0:48, :], Act.Copy, [t], scale=0.25)
     for buf, c in ((T.iy, -96.0), (T.ix, -1.0)):
         tis = act(buf[:], T.ident[:], Act.Copy, [tid], scale=c)
+    trep = act(T.rep4[0:48, :], T.rep[0:48, :], Act.Copy, [t], scale=0.25)
 
     ts(T.smb[0:8, 64:128], T.ints[0:8, 64:128], -1.0, 240.0, Op.mult, Op.add, deps=[lds])
     tb = ts(T.smb[0:8, 128:160], T.ints[0:8, 128:160], 128.0, None, Op.add)
     tsx = ts(T.smb[0:8, 0:64], T.ints[0:8, 0:64], -1.0 / 16, None, Op.mult)
+    fill(T.cb[0:32, 8:9], -128.0)
+    fill(T.cb[0:32, 9:10], -1.0)
+    fill(T.cb[0:32, 11:12], 69.0)
+    tcb = fill(T.cb[32:64, 11:12], 15.0 / 32)
     for h in range(NH):
         for e in range(4):
             for blk in range(2):
                 c0, wd = 64 + 32 * min(e, 2) + 16 * h, 32 - 16 * blk
-                tm0 = mm(pA[0][32 * blk:32 * blk + wd, 16 * h + e:16 * h + 16:4], T.smb[0:8, c0:c0 + wd],
+                tm0 = mm(pA[0][32 * blk:32 * blk + wd, 0, 16 * h + e:16 * h + 16:4], T.smb[0:8, c0:c0 + wd],
                          T.ident[0:8, blk:8:2], True, True, [tb])
     for tbl in range(2):
         for s in range(4):
@@ -155,27 +155,27 @@ def rank_program(g, core, T, topo):
                 c0 = 32 * tbl + 8 * s + 4 * kk
                 tm1 = mm(pC[1][:, c0:c0 + 4], T.mkt[0:8, :], T.smb[0:8, 32 * tbl + 2 * s + kk:32 * tbl + 32:8],
                          True, True, [tsx])
+    t = cp(M[0:48, 2:NH * DT:3], pA[0][0:48, 0, 0:32], [tm0])
+    ts(M[0:48, 9:NH * DT:L], pA[0][0:48, 0, 2:32:4], 139.0, None, Op.max)
+    ts(M[0:48, 10:NH * DT:L], pA[0][0:48, 0, 2:32:4], 140.0, None, Op.max)
+    td0 = ts(M[0:48, 11:NH * DT:L], pA[0][0:48, 0, 2:32:4], 151.0, 152.0, Op.max, Op.min, deps=[t])
     for c, sign in ((0, 1), (3, 1), (6, -1)):
         fill(T.ca[32:64, c:DT:L], sign * 33.0 / 64)
     fill(T.seg[:, 0:256:4], 0.0)
-    t = cp(M[0:48, 2:NH * DT:3], pA[0][0:48, 0:32], [tm0])
-    ts(M[0:48, 9:NH * DT:L], pA[0][0:48, 2:32:4], 139.0, None, Op.max)
-    ts(M[0:48, 10:NH * DT:L], pA[0][0:48, 2:32:4], 140.0, None, Op.max)
-    cp(T.sxy[:], pC[1][:, 0:64], [tm1])
-    tsxy = td0 = ts(M[0:48, 11:NH * DT:L], pA[0][0:48, 2:32:4], 151.0, 152.0, Op.max, Op.min, deps=[t])
-    act(T.h4[:, 0:16], T.hd[:, 0:16], Act.Copy, [lds], scale=-1.0 / 512)
+    tsxy = cp(T.sxy[:], pC[1][:, 0:64], [tm1])
+    act(T.h4[:, 0:16], T.hd[:, 0:16], Act.Copy, [ldh], scale=-1.0 / 512)
     act(T.h4[:, 16:24], T.hd[:, 16:24], Act.Copy, scale=1.0 / 512)
     t = act(T.h4[:, 24:32], T.hd[:, 16:24], Act.Copy, scale=0.0)
     for gi in range(8):
         c0 = 128 * (gi % 2) + 32 * (gi // 2)
         twt = act(T.wt[:, c0:c0 + 32], T.h4[:], Act.Identity, [t, tmk], scale=T.mk[:, gi:gi + 1])
 
-    last = [{"upd": tsxy, "off": tsxy, "lev": tsxy} for _ in range(NH)]
+    last = [{"upd": td0, "off": tsxy, "lev": tcb} for _ in range(NH)]
 
     def open_state(h, level=True):
         mm(pB[h][:, 0:L], T.ones[0:64, :], T.cb[0:64, :], True, False, [last[h]["lev"]])
         if level:
-            mm(pD[h][:, 0:1], T.ones[0:32, :], T.cd[0:32, 0:1], True, False)
+            mm(pD[h][:, 0, 0:1], T.ones[0:32, :], T.cd[0:32, 0:1], True, False)
 
     def open_offsets(h):
         mm(pC[h][:, 0:32], T.ones[0:96, :], T.cc[0:96, :], True, False, [last[h]["off"]])
@@ -187,8 +187,8 @@ def rank_program(g, core, T, topo):
             tb_ = mm(pB[h][32 * qd:32 * qd + 32, 0:L], T.rep[0:48, :], M[0:48, s + L * qd:s + L * qd + L], False, True, deps)
         td = None
         for qd in range(4 if level else 0):
-            td = mm(pD[h][32 * qd:32 * qd + 32, 0:1], T.rep4[0:48, :], M[0:48, s + L * qd + 11:s + L * qd + 12], False, True,
-                    [trep])
+            td = mm(pD[h][32 * qd:32 * qd + 32, 0, 0:1], T.rep4[0:48, :], M[0:48, s + L * qd + 11:s + L * qd + 12],
+                    False, True, [trep])
         return tb_, td
 
     def clamp(h, st, tb_):
@@ -197,7 +197,7 @@ def rank_program(g, core, T, topo):
     def begin(h, st, tn):
         tq = ts(T["q%d" % h][:], T.sxy[:], pB[h][:, 8:9], pB[h][:, 11:12], Op.mult, Op.add, deps=[tn[0], tsxy])
         txy = clamp(h, st, tn[0])
-        last[h]["lev"] = ts(T["f%d" % h][:], pB[h][:, 9:10], pB[h][:, 10:11], pD[h][:, 0:1], Op.subtract, Op.mult,
+        last[h]["lev"] = ts(T["f%d" % h][:], pB[h][:, 9:10], pB[h][:, 10:11], pD[h][:, 0, 0:1], Op.subtract, Op.mult,
                             deps=[tn[1]])
         return tq, txy
 
@@ -217,25 +217,28 @@ def rank_program(g, core, T, topo):
         act(T.lo[0:48, DT * h + 7:DT * h + DT:L], M[0:48, s + 8:s + DT:L], Act.Identity,
             list(deps) + [last[h]["upd"]], bias=-12.0)
 
-    def open_head(h, s):
-        mm(pA[h][0:48, 0:DT], T.ones[0:63, 0:48], T.ca[0:63, :], True, False, [last[h]["upd"], tca])
+    def open_head(h, s, deps=()):
+        mm(pA[h][0:48, 0, 0:DT], T.ones[0:63, 0:48], T.ca[0:63, :], True, False, [last[h]["upd"], tca] + list(deps))
         for c in (6, 7):
-            mm(pA[h][0:48, c:DT:L], T.ident[0:48, 0:48], M[0:48, s + 8:s + DT:L], False, False)
+            mm(pA[h][0:48, 0, c:DT:L], T.ident[0:48, 0:48], M[0:48, s + 8:s + DT:L], False, False)
 
-    def gathers(h, ready):
+    def gathers(h, ready, between=None):
         off, ga = T["off%d" % h], T["ga%d" % h]
         deps = [last[h]["off"]] + ready
         for s in (0, 1):
             ta = act(ga[:, s:512:4], T.win[:].indirect(off[:, 8 * s:8 * s + 8]), Act.Copy, deps)
         for s in (2, 3):
             tv = cp(ga[:, s:512:4], T.win[:].indirect(off[:, 8 * s:8 * s + 8]), deps)
+            if between and s == 2:
+                between()
         return ta, tv
 
     def pool(h, tg):
         ga, gb = T["ga%d" % h], T["gb%d" % h]
-        tk = [None, None]
-        for k in (1, 0):
-            tk[k] = scan(gb[:, 256 * k:256 * k + 256], T.seg[:], ga[:, 256 * k:256 * k + 256], Op.mult, Op.max, tg)
+        tk = {}
+        for b0, b1 in ((5, 8), (2, 5), (0, 2)):
+            t = scan(gb[:, 64 * b0:64 * b1], T.seg[:, 0:64 * (b1 - b0)], ga[:, 64 * b0:64 * b1], Op.mult, Op.max, tg)
+            tk.update({b: t for b in range(b0, b1)})
         return tk
 
     def head(h, tk):
@@ -243,44 +246,58 @@ def rank_program(g, core, T, topo):
         for b in range(7, -1, -1):
             for blk in range(2):
                 wd = 128 if b == 0 and blk == 0 else 64
-                m1 = mm(pA[h][32 * blk:32 * blk + wd // 4, 0:DT:3], gb[:, 64 * b + 3:64 * b + wd:4],
-                        T.wt[:, 128 * blk + b:128 * blk + 128:8], False, b == 0, [tk[b // 4], twt])
+                m1 = mm(pA[h][32 * blk:32 * blk + wd // 4, 0, 0:DT:3], gb[:, 64 * b + 3:64 * b + wd:4],
+                        T.wt[:, 128 * blk + b:128 * blk + 128:8], False, b == 0, [tk[b], twt])
         return m1
 
     def update(h, j, m1):
         s0 = slot(h, j - 1)
-        last[h]["upd"] = scan(M[0:48, s0:s0 + DT], T.lo[0:48, DT * h:DT * h + DT], pA[h][0:48, 0:DT], Op.max, Op.min,
+        last[h]["upd"] = scan(M[0:48, s0:s0 + DT], T.lo[0:48, DT * h:DT * h + DT], pA[h][0:48, 0, 0:DT], Op.max, Op.min,
                               [m1, tlo])
         w = DT if j == NV - 1 else DT + 4 * j
         send(M[:, slot(h, j):slot(h, j) + w], M[:, s0:s0 + w], "arr%d_%d" % (h, j), [last[h]["upd"]])
 
     sts = [lambda a, b, h=h: T.est[:, 4 * h + a:4 * h + b] for h in range(NH)]
     mids = []
+    pieces = [(24, 2304 + 96 * k, 2280 + 384 * k) for k in range(6)] + \
+             [(48, 192 * k, 4608 + 384 * k) for k in range(RV // 4, 12)]
+    free = [(pA[1], td0), (pA[0], td0)]
+
+    def repeat(count):
+        for _ in range(count):
+            (wd, src, dst), (ps, read) = pieces.pop(0), free.pop(0)
+            for c in range(0, 96, wd):
+                t = mm(ps[:, :, c:c + wd], T.ident[:], T.raw[:, src:src + 4 * wd], True, True, [ld1, read])
+            t = act(T.win[:, dst:dst + 384], ps[:, :, 0:96], Act.Copy, [t])
+            free.append((ps, t))
+        return t
+
     for h in range(NH):
         open_state(h)
-        open_offsets(h)
+        bounds(h, slot(h, -1), [td0])
     tns = [turn(h, slot(h, -1), None, [td0]) for h in range(NH)]
+    repeat(2)
+    for h in range(NH):
+        open_offsets(h)
     for h in range(NH):
         mids.append(begin(h, sts[h], tns[h]))
-        bounds(h, slot(h, -1), [td0])
     send(T.eland[:], T.est[:], "early", [mids[1][1]])
+    tcs = [corner(h, sts[h], mids[h][1]) for h in range(NH)]
+    for k in range(2):
+        tv = cp(T.s1[:, :, k, :], T.raw[:, 0:48 * RV], [ld1])
+    free[0:0] = [(pD[h], last[h]["lev"]) for h in range(NH)]
+    repeat(2)
     for h in range(NH):
-        offsets(h, corner(h, sts[h], mids[h][1]), mix(h, mids[h][0]))
+        offsets(h, tcs[h], mix(h, mids[h][0]))
+    ev = cp(T.win[:, 4608:4608 + 96 * RV], T.s1[:], [tv])
+    ea = repeat(len(pieces))
     for h in range(NH):
-        open_head(h, slot(h, -1))
+        open_head(h, slot(h, -1), [ea])
+    for h in range(NH):
         open_state(h)
         open_offsets(h)
-    for k in range(4):
-        t = act(T.s2[:, :, k, :], T.win[:, 2304:2880], Act.Copy, [ld1])
-    for k in range(2):
-        tv = cp(T.s1[:, :, k, :], T.win[:, 0:2304], [ld1])
-    ea = act(T.win[:, 2280:4584], T.s2[:], Act.Copy, [t, tv])
-    ev = cp(T.win[:, 4608:9216], T.s1[:], [tv])
-    tg0 = gathers(0, [ld0, ld1, ea, ev])
-    tk0 = pool(0, tg0)
-    tg1 = gathers(1, [])
-    update(0, 0, head(0, tk0))
-    pend = (1, 0, pool(1, tg1))
+    m1 = head(0, pool(0, gathers(0, [ld0, ea, ev])))
+    pend = (1, 0, pool(1, gathers(1, [], lambda: update(0, 0, m1))))
 
     def arrival(h, j, level=True):
         s = slot(h, j)
@@ -330,10 +347,10 @@ def rank_program(g, core, T, topo):
     for h in range(NH):
         for e in range(3):
             for b in range(16):
-                th = mm(pA[h][0:8, 128 * e + b:128 * e + 112:16], T.ident[:, b:128:16], T["hl%d" % h][:, e:28:4],
+                th = mm(pA[h][0:8, e, b:112:16], T.ident[:, b:128:16], T["hl%d" % h][:, e:28:4],
                         True, True, [last[h]["upd"], ("hist%d" % h, n_in)])
         for e in range(3):
-            te = act(T.tr[0:8, e:21:3, 16 * h:16 * h + 16], pA[h][0:8, 128 * e:128 * e + 112], Act.Identity, [th],
+            te = act(T.tr[0:8, e:21:3, 16 * h:16 * h + 16], pA[h][0:8, e, 0:112], Act.Identity, [th],
                      bias=96.0 if e < 2 else 0.0, scale=-1.0 if e < 2 else 1.0)
     wait("sy", te)
     g.sync.dma_start(T.trail[:, 0:672], T.tr[0:8, 0:21, :]).then_inc(T.sem.st1, 16)

from concourse.mybir import AluOpType as Op, ActivationFunctionType as Act

NH = 2
NV = 8
L = 12
DT = 4 * L
WS = DT + 32
RV = 36
BIG = 1024
INTER = (0, 1)


def slot(h, j):
    return h * DT if j < 0 else NH * DT + (h * NV + j) * WS


SCRATCH = {"s1": ("sbuf", [128, RV, 2, 48], "bfloat16"),
           "fo": ("sbuf", [128, 8, 32], "bfloat16"), "tr": ("sbuf", [128, 24, 32], "float32"),
           "ints": ("sbuf", [128, 160], "int32")}
for _n, _c in dict(win=18432, raw=2880, hd=24, h4=32, wt=256, smb=176, ident=128, iy=128, ix=128, ones=128,
                   mkt=128, rep=32, rep4=32, sxy=64, ca=DT, cb=L, cc=32, cd=2, ct=48, est=8, eland=8, fland=256,
                   msg=NH * (DT + NV * WS), seg=256, q0=64, q1=64, lo=NH * DT, ga0=512, ga1=512, gb0=512, gb1=512,
                   hl0=28, hl1=28).items():
    SCRATCH[_n] = ("sbuf", [128, _c], "bfloat16")
for _n, _c in dict(dio=128, dio2=128, mkc=8, mk=8, f0=1, f1=1, base0=1, base1=1).items():
    SCRATCH[_n] = ("sbuf", [128, _c], "float32")
for _h in range(NH):
    SCRATCH["off%d" % _h] = ("sbuf", [128, 32], "uint16")
    for _n in "ABCD":
        SCRATCH["ps%s%d" % (_n, _h)] = ("psum", [128, 4, 128] if _n in "AD" else [128, 512], "float32")

SEMAPHORES = ["v", "a", "pe", "gp", "lds", "ldh", "ld1", "ld0", "early", "loc", "st1", "st2", "hist0", "hist1", "fin"] + \
             ["arr%d_%d" % (h, j) for h in range(NH) for j in range(NV)]


def rank_program(g, core, T, topo):
    rank = T.rank_of(core)
    if rank is None:
        return
    n = len(T.cores)
    nxt, prv = T.cores[(rank + 1) % n], T.cores[(rank - 1) % n]
    rid, pid, _ = topo.addr(nxt)
    mask = topo.mask(core, nxt)
    n_out, n_in = len(topo.engines(core, nxt)), len(topo.engines(prv, core))

    Q = {"v": g.vector, "a": g.scalar, "pe": g.tensor, "gp": g, "sy": g.sync}
    cnt = {"v": 0, "a": 0, "pe": 0, "gp": 0, "loc": 0}
    seen = {}

    def wait(q, *tickets):
        for t in tickets:
            if t is not None and seen.get((q, t[0]), 0) < t[1]:
                Q[q].wait_ge(T.sem[t[0]], t[1])
                seen[(q, t[0])] = t[1]

    def done(q, inst):
        inst.then_inc(T.sem[q], 1)
        cnt[q] += 1
        return (q, cnt[q])

    def ts(out, in0, s1, s2, op0, op1=None, deps=()):
        wait("v", *deps)
        if op1 is None:
            return done("v", g.vector.tensor_scalar(out, in0, s1, None, op0))
        return done("v", g.vector.tensor_scalar(out, in0, s1, s2, op0, op1))

    def tt(out, a, b, op, deps=()):
        wait("v", *deps)
        return done("v", g.vector.tensor_tensor(out, a, b, op))

    def cp(out, a, deps=()):
        wait("v", *deps)
        return done("v", g.vector.tensor_copy(out, a))

    def scan(out, a, b, op0, op1, deps=()):
        wait("v", *deps)
        return done("v", g.vector.tensor_tensor_scan(out, a, b, 0.0, op0, op1))

    def fill(ap, c, deps=()):
        wait("v", *deps)
        return done("v", g.vector.memset(ap, c))

    def mm(out, lhsT, rhs, start, stop, deps=()):
        wait("pe", *deps)
        return done("pe", g.tensor.matmul(out, lhsT, rhs, start, stop))

    def act(out, in_, func, deps=(), **kw):
        wait("a", *deps)
        return done("a", g.scalar.activation(out, in_, func, **kw))

    def const(ap, cols, c):
        return done("gp", g.iota(ap, [[0, cols]], c, 0, allow_small_or_imprecise_dtypes=True))

    def send(dst, src, sem, deps):
        wait("gp", *deps)
        g.remote_dma(dst, src, T.sem[sem], T.sem.loc, pid, rid, mask)
        cnt["loc"] += n_out

    M = T.msg
    pA, pB, pC, pD = ([T["ps%s%d" % (b, h)] for h in range(NH)] for b in "ABCD")

    g.scalar.dma_start(T.ints[0:8, 64:160], T.box[:]).then_inc(T.sem.lds, 16)
    g.scalar.dma_start(T.ints[0:8, 0:32], T.sy[:]).then_inc(T.sem.lds, 16)
    g.sync.dma_start(T.ints[0:8, 32:64], T.sx[:]).then_inc(T.sem.lds, 16)
    g.sync.dma_start(T.hd[:], T.head[:]).then_inc(T.sem.ldh, 16)
    g.sync.dma_start(T.raw[:], T.pyr[:, 9216:12096]).then_inc(T.sem.ld1, 16)
    g.sync.dma_start(T.win[:, 9216:18432], T.pyr[:, 0:9216]).then_inc(T.sem.ld0, 16)
    lds, ldh, ld1, ld0 = ("lds", 48), ("ldh", 16), ("ld1", 16), ("ld0", 16)

    io1 = done("gp", g.iota(T.dio[:], [[-1, 128]], 0, 1, allow_small_or_imprecise_dtypes=True))
    io2 = done("gp", g.iota(T.dio2[0:8, :], [[1, 8], [0, 16]], 0, -1, allow_small_or_imprecise_dtypes=True))
    for c, val in enumerate((144, 156, BIG, 144, 156, BIG, 0, 12, 216, BIG, BIG, 152)):
        tca = const(T.ca[0:32, c:DT:L], 4, val)
    for c, val in enumerate((BIG, 132, -BIG, BIG, 132, -BIG, BIG, None, 132, 139, 140, 151)):
        if val is not None:
            tlo = const(T.lo[0:48, c:NH * DT:L], 4 * NH, val)
    fill(T.ones[:], 1.0 / 32)
    fill(T.rep[0:64, :], 0.0)
    fill(M[:, 0:NH * DT], 0.0)
    fill(T.smb[0:8, 160:176], 0.0)
    fill(T.cb[0:64, :], 0.0)
    fill(T.ca[32:64, :], 0.0)
    fill(T.seg[:], 1.0)
    tid = ts(T.ident[:], T.dio[:], 0.0, None, Op.is_equal, deps=[io1])
    t = ts(T.mkc[:], T.dio[:, 0:128:16], 0.0, 15.0, Op.max, Op.min)
    fill(T.cc[0:32, :], 39936.0)
    fill(T.cc[32:64, :], -68.0)
    tmk = tt(T.mk[:], T.mkc[:], T.dio[:, 0:128:16], Op.is_equal, [t])
    cp(T.rep[0:16, 0:16], T.ident[0:16, 0:16])
    t = cp(T.rep[32:48, 16:32], T.ident[32:48, 32:48])
    ts(T.mkt[0:8, :], T.dio2[0:8, :], 0.0, None, Op.is_equal, deps=[io2])
    fill(T.cc[64:96, :], -0.25)
    fill(T.cd[0:32, :], -38.25)
    fill(T.cb[0:32, 2:6:3], -144.0)
    for buf, c in ((T.iy, -96.0), (T.ix, -1.0)):
        tis = act(buf[:], T.ident[:], Act.Copy, [tid], scale=c)
    trep = act(T.rep4[0:48, :], T.rep[0:48, :], Act.Copy, [t], scale=0.25)

    ts(T.smb[0:8, 64:128], T.ints[0:8, 64:128], -1.0, 240.0, Op.mult, Op.add, deps=[lds])
    tb = ts(T.smb[0:8, 128:160], T.ints[0:8, 128:160], 128.0, None, Op.add)
    tsx = ts(T.smb[0:8, 0:64], T.ints[0:8, 0:64], -1.0 / 16, None, Op.mult)
    fill(T.cb[0:32, 8:9], -128.0)
    fill(T.cb[0:32, 9:10], -1.0)
    fill(T.cb[0:32, 11:12], 69.0)
    tcb = fill(T.cb[32:64, 11:12], 15.0 / 32)
    for h in range(NH):
        for e in range(4):
            for blk in range(2):
                c0, wd = 64 + 32 * min(e, 2) + 16 * h, 32 - 16 * blk
                tm0 = mm(pA[0][32 * blk:32 * blk + wd, 0, 16 * h + e:16 * h + 16:4], T.smb[0:8, c0:c0 + wd],
                         T.ident[0:8, blk:8:2], True, True, [tb])
    for tbl in range(2):
        for s in range(4):
            for kk in range(2):
                c0 = 32 * tbl + 8 * s + 4 * kk
                tm1 = mm(pC[1][:, c0:c0 + 4], T.mkt[0:8, :], T.smb[0:8, 32 * tbl + 2 * s + kk:32 * tbl + 32:8],
                         True, True, [tsx])
    t = cp(M[0:48, 2:NH * DT:3], pA[0][0:48, 0, 0:32], [tm0])
    ts(M[0:48, 9:NH * DT:L], pA[0][0:48, 0, 2:32:4], 139.0, None, Op.max)
    ts(M[0:48, 10:NH * DT:L], pA[0][0:48, 0, 2:32:4], 140.0, None, Op.max)
    td0 = ts(M[0:48, 11:NH * DT:L], pA[0][0:48, 0, 2:32:4], 151.0, 152.0, Op.max, Op.min, deps=[t])
    for c, sign in ((0, 1), (3, 1), (6, -1)):
        fill(T.ca[32:64, c:DT:L], sign * 33.0 / 64)
    fill(T.seg[:, 0:256:4], 0.0)
    tsxy = cp(T.sxy[:], pC[1][:, 0:64], [tm1])
    act(T.h4[:, 0:16], T.hd[:, 0:16], Act.Copy, [ldh], scale=-1.0 / 512)
    act(T.h4[:, 16:24], T.hd[:, 16:24], Act.Copy, scale=1.0 / 512)
    t = act(T.h4[:, 24:32], T.hd[:, 16:24], Act.Copy, scale=0.0)
    for gi in range(8):
        c0 = 128 * (gi % 2) + 32 * (gi // 2)
        twt = act(T.wt[:, c0:c0 + 32], T.h4[:], Act.Identity, [t, tmk], scale=T.mk[:, gi:gi + 1])

    last = [{"upd": td0, "off": tsxy, "lev": tcb} for _ in range(NH)]

    def open_state(h, level=True):
        mm(pB[h][:, 0:L], T.ones[0:64, :], T.cb[0:64, :], True, False, [last[h]["lev"]])
        if level:
            mm(pD[h][:, 0, 0:1], T.ones[0:32, :], T.cd[0:32, 0:1], True, False)

    def open_offsets(h):
        mm(pC[h][:, 0:32], T.ones[0:96, :], T.cc[0:96, :], True, False, [last[h]["off"]])

    def turn(h, s, prev, deps, level=True):
        if prev is not None:
            mm(pB[h][:, 2:6:3], T.ident[:], prev, False, False, deps)
        for qd in range(4):
            tb_ = mm(pB[h][32 * qd:32 * qd + 32, 0:L], T.rep[0:48, :], M[0:48, s + L * qd:s + L * qd + L], False, True, deps)
        td = None
        for qd in range(4 if level else 0):
            td = mm(pD[h][32 * qd:32 * qd + 32, 0, 0:1], T.rep4[0:48, :], M[0:48, s + L * qd + 11:s + L * qd + 12],
                    False, True, [trep])
        return tb_, td

    def clamp(h, st, tb_):
        return ts(st(0, 4), pB[h][:, 2:L:3], pB[h][:, 8:9], 96.0, Op.max, Op.min, deps=[tb_])

    def begin(h, st, tn):
        tq = ts(T["q%d" % h][:], T.sxy[:], pB[h][:, 8:9], pB[h][:, 11:12], Op.mult, Op.add, deps=[tn[0], tsxy])
        txy = clamp(h, st, tn[0])
        last[h]["lev"] = ts(T["f%d" % h][:], pB[h][:, 9:10], pB[h][:, 10:11], pD[h][:, 0, 0:1], Op.subtract, Op.mult,
                            deps=[tn[1]])
        return tq, txy

    def mix(h, tq):
        qb = T["q%d" % h]
        mm(pC[h][:, 0:32], T.iy[:], qb[:, 0:32], False, False, [tq, tis])
        return mm(pC[h][:, 0:32], T.ix[:], qb[:, 32:64], False, True)

    def corner(h, st, txy):
        return ts(T["base%d" % h][:], st(1, 2), -96.0, st(0, 1), Op.mult, Op.subtract, deps=[txy])

    def offsets(h, tc, m3):
        last[h]["off"] = ts(T["off%d" % h][:], pC[h][:, 0:32], T["base%d" % h][:], T["f%d" % h][:], Op.add, Op.mult,
                            deps=[tc, m3])

    def bounds(h, s, deps):
        act(T.lo[0:48, DT * h + 7:DT * h + DT:L], M[0:48, s + 8:s + DT:L], Act.Identity,
            list(deps) + [last[h]["upd"]], bias=-12.0)

    def open_head(h, s, deps=()):
        mm(pA[h][0:48, 0, 0:DT], T.ones[0:63, 0:48], T.ca[0:63, :], True, False, [last[h]["upd"], tca] + list(deps))
        for c in (6, 7):
            mm(pA[h][0:48, 0, c:DT:L], T.ident[0:48, 0:48], M[0:48, s + 8:s + DT:L], False, False)

    def gathers(h, ready, between=None):
        off, ga = T["off%d" % h], T["ga%d" % h]
        deps = [last[h]["off"]] + ready
        for s in (0, 1):
            ta = act(ga[:, s:512:4], T.win[:].indirect(off[:, 8 * s:8 * s + 8]), Act.Copy, deps)
        for s in (2, 3):
            tv = cp(ga[:, s:512:4], T.win[:].indirect(off[:, 8 * s:8 * s + 8]), deps)
            if between and s == 2:
                between()
        return ta, tv

    def pool(h, tg):
        ga, gb = T["ga%d" % h], T["gb%d" % h]
        tk = {}
        for b0, b1 in ((5, 8), (2, 5), (0, 2)):
            t = scan(gb[:, 64 * b0:64 * b1], T.seg[:, 0:64 * (b1 - b0)], ga[:, 64 * b0:64 * b1], Op.mult, Op.max, tg)
            tk.update({b: t for b in range(b0, b1)})
        return tk

    def head(h, tk):
        gb = T["gb%d" % h]
        for b in range(7, -1, -1):
            for blk in range(2):
                wd = 128 if b == 0 and blk == 0 else 64
                m1 = mm(pA[h][32 * blk:32 * blk + wd // 4, 0, 0:DT:3], gb[:, 64 * b + 3:64 * b + wd:4],
                        T.wt[:, 128 * blk + b:128 * blk + 128:8], False, b == 0, [tk[b], twt])
        return m1

    def update(h, j, m1):
        s0 = slot(h, j - 1)
        last[h]["upd"] = scan(M[0:48, s0:s0 + DT], T.lo[0:48, DT * h:DT * h + DT], pA[h][0:48, 0, 0:DT], Op.max, Op.min,
                              [m1, tlo])
        w = DT if j == NV - 1 else DT + 4 * j
        send(M[:, slot(h, j):slot(h, j) + w], M[:, s0:s0 + w], "arr%d_%d" % (h, j), [last[h]["upd"]])

    sts = [lambda a, b, h=h: T.est[:, 4 * h + a:4 * h + b] for h in range(NH)]
    mids = []
    pieces = [(24, 2304 + 96 * k, 2280 + 384 * k) for k in range(6)] + \
             [(48, 192 * k, 4608 + 384 * k) for k in range(RV // 4, 12)]
    free = [(pA[1], td0), (pA[0], td0)]

    def repeat(count):
        for _ in range(count):
            (wd, src, dst), (ps, read) = pieces.pop(0), free.pop(0)
            for c in range(0, 96, wd):
                t = mm(ps[:, :, c:c + wd], T.ident[:], T.raw[:, src:src + 4 * wd], True, True, [ld1, read])
            t = act(T.win[:, dst:dst + 384], ps[:, :, 0:96], Act.Copy, [t])
            free.append((ps, t))
        return t

    for h in range(NH):
        open_state(h)
        bounds(h, slot(h, -1), [td0])
    tns = [turn(h, slot(h, -1), None, [td0]) for h in range(NH)]
    repeat(2)
    for h in range(NH):
        open_offsets(h)
    for h in range(NH):
        mids.append(begin(h, sts[h], tns[h]))
    send(T.eland[:], T.est[:], "early", [mids[1][1]])
    tcs = [corner(h, sts[h], mids[h][1]) for h in range(NH)]
    for k in range(2):
        tv = cp(T.s1[:, :, k, :], T.raw[:, 0:48 * RV], [ld1])
    free[0:0] = [(pD[h], last[h]["lev"]) for h in range(NH)]
    repeat(2)
    for h in range(NH):
        offsets(h, tcs[h], mix(h, mids[h][0]))
    ev = cp(T.win[:, 4608:4608 + 96 * RV], T.s1[:], [tv])
    ea = repeat(len(pieces))
    for h in range(NH):
        open_head(h, slot(h, -1), [ea])
    for h in range(NH):
        open_state(h)
        open_offsets(h)
    m1 = head(0, pool(0, gathers(0, [ld0, ea, ev])))
    pend = (1, 0, pool(1, gathers(1, [], lambda: update(0, 0, m1))))

    def arrival(h, j, level=True):
        s = slot(h, j)
        arr = ("arr%d_%d" % (h, j), n_in)
        if j == 0:
            prev, known = T.eland[:, 4 * h:4 * h + 2], ("early", n_in)
        elif j == NV - 1:
            prev, known = T["hl%d" % h][:, 24:26], ("hist%d" % h, n_in)
        else:
            prev, known = M[:, s + DT + 4 * j - 4:s + DT + 4 * j - 2], arr
        st = lambda a, b: M[:, s + DT + 4 * j + a:s + DT + 4 * j + b]
        if level:
            bounds(h, s, [arr])
        return st, turn(h, s, prev, [known, arr], level)

    def keep_feats(h, tk):
        return act(T.fo[:, :, 16 * h:16 * h + 16], T["gb%d" % h][:, 3:512:4], Act.Copy, [tk[0]])

    for j in range(NV - 1):
        for h in range(NH):
            if not INTER[h]:
                m1 = head(pend[0], pend[2])
            st, tn = arrival(h, j)
            if INTER[h]:
                m1 = head(pend[0], pend[2])
            else:
                update(pend[0], pend[1], m1)
            tq, txy = begin(h, st, tn)
            m3 = mix(h, tq)
            tc = corner(h, st, txy)
            if INTER[h]:
                update(pend[0], pend[1], m1)
            offsets(h, tc, m3)
            open_head(h, slot(h, j))
            open_state(h, j < NV - 2)
            if j < NV - 2:
                open_offsets(h)
            pend = (h, j + 1, pool(h, gathers(h, [])))
            if j == NV - 2:
                send(T["hl%d" % h][:], M[:, slot(h, j) + DT:slot(h, j) + DT + 28], "hist%d" % h, [last[h]["off"]])
                tf = keep_feats(h, pend[2])
    update(pend[0], pend[1], head(pend[0], pend[2]))
    send(T.fland[:], T.fo[:], "fin", [tf])

    fill(T.ct[0:32, 0:32], -96.0)
    tct = fill(T.ct[0:32, 32:48], 0.0)
    for h in range(NH):
        for e in range(3):
            for b in range(16):
                th = mm(pA[h][0:8, e, b:112:16], T.ident[:, b:128:16], T["hl%d" % h][:, e:28:4],
                        True, True, [last[h]["upd"], ("hist%d" % h, n_in)])
        for e in range(3):
            te = act(T.tr[0:8, e:21:3, 16 * h:16 * h + 16], pA[h][0:8, e, 0:112], Act.Identity, [th],
                     bias=96.0 if e < 2 else 0.0, scale=-1.0 if e < 2 else 1.0)
    wait("sy", te)
    g.sync.dma_start(T.trail[:, 0:672], T.tr[0:8, 0:21, :]).then_inc(T.sem.st1, 16)
    for h in range(NH):
        mm(pC[h][0:8, 0:48], T.ones[0:32, 0:8], T.ct[0:32, :], True, False, [tct])
    for h in range(NH):
        st, tn = arrival(h, NV - 1, False)
        txy = clamp(h, st, tn[0])
        for b in range(16):
            tl = mm(pC[h][0:8, b:48:16], T.ident[:, b:128:16], st(0, 3), False, b == 15, [txy])
        tz = act(T.tr[0:8, 21:24, 16 * h:16 * h + 16], pC[h][0:8, 0:48], Act.Abs, [tl])
    wait("sy", ("fin", n_in))
    g.sync.dma_start(T.feat[:], T.fland[:]).then_inc(T.sem.st1, 16)
    wait("a", tz)
    g.scalar.dma_start(T.trail[:, 672:768], T.tr[0:8, 21:24, :]).then_inc(T.sem.st2, 16)
    wait("gp", ("loc", cnt["loc"]), ("v", cnt["v"]), ("a", cnt["a"]), ("pe", cnt["pe"]), ("gp", cnt["gp"]),
         ("st1", 32), ("st2", 16))
